import numpy as np
CORES = [1,129,9,137,17,145,25,153,33,161,41,169,49,177,57,185,65,193,73,201,81,209,89,217,97,225,105,233,113,241,121,249]
N = 32
T = 256
ROUTE = [[[15,30],[15,18],[29,15],[2,15],[18,21],[29,2],[23,11],[9,20],[28,4],[15,10],[30,26],[29,30],[5,15],[3,27],[15,17],[15,9],[26,5],[15,6],[15,23],[31,2],[15,21],[17,15],[15,18],[15,17],[4,15],[15,18],[15,16],[16,15],[10,15],[15,30],[15,14],[15,1],[7,15],[31,15],[15,16],[17,0],[19,15],[15,8],[10,9],[17,15],[15,4],[15,25],[15,17],[27,15],[15,22],[0,21],[4,1],[21,4],[15,12],[15,16],[28,15],[15,16],[15,2],[15,16],[8,20],[15,4],[12,17],[15,8],[8,15],[28,15],[15,30],[5,15],[15,16],[15,10],[15,16],[14,27],[15,23],[30,15],[9,15],[15,21],[13,15],[15,17],[29,24],[9,15],[15,1],[25,15],[15,28],[15,9],[20,10],[15,7],[15,27],[15,2],[15,2],[15,18],[15,23],[13,15],[9,20],[15,30],[25,3],[15,17],[13,15],[7,9],[11,15],[13,8],[22,13],[12,27],[27,15],[23,15],[15,5],[20,22],[15,17],[17,15],[7,14],[15,13],[15,23],[5,13],[15,19],[15,30],[15,3],[15,18],[12,15],[4,18],[15,27],[18,15],[27,15],[3,2],[19,27],[15,18],[6,15],[15,26],[9,6],[15,19],[15,14],[15,8],[17,14],[13,20],[15,29],[15,22],[7,3],[15,13],[3,20],[1,15],[21,2],[15,4],[27,15],[10,14],[11,0],[15,7],[25,15],[18,26],[2,8],[9,0],[15,29],[0,8],[14,9],[20,9],[25,15],[17,15],[13,15],[15,28],[15,21],[4,9],[15,24],[15,0],[15,30],[15,21],[2,27],[16,12],[20,27],[0,6],[16,14],[4,15],[15,31],[23,15],[12,15],[21,15],[15,26],[12,10],[9,8],[15,6],[27,12],[15,17],[21,15],[27,15],[31,15],[14,17],[18,10],[24,11],[15,8],[15,29],[15,6],[24,29],[14,18],[27,3],[15,8],[12,15],[0,3],[12,15],[15,18],[1,15],[15,2],[7,13],[15,29],[29,6],[23,15],[12,30],[15,12],[15,18],[15,0],[9,15],[6,22],[19,15],[10,15],[15,1],[4,0],[1,10],[28,25],[13,16],[28,15],[15,24],[4,15],[8,19],[29,30],[15,28],[21,15],[15,23],[12,26],[18,15],[15,29],[15,2],[20,6],[15,6],[15,2],[15,25],[11,15],[15,26],[15,20],[12,15],[11,21],[9,26],[15,3],[16,20],[20,15],[21,10],[27,23],[15,24],[15,2],[9,29],[15,27],[14,21],[3,27],[15,5],[15,27],[15,17],[15,25],[25,0],[18,12],[17,4],[30,15],[1,22],[29,17],[15,0],[15,24],[2,3],[20,15],[19,15]],[[2,24],[20,15],[15,2],[8,26],[15,25],[15,0],[23,14],[15,24],[8,2],[3,15],[17,31],[22,13],[15,8],[10,15],[16,15],[1,25],[26,30],[16,26],[17,0],[12,15],[15,2],[15,16],[17,29],[15,0],[15,18],[13,15],[5,29],[15,16],[0,6],[22,11],[15,8],[15,19],[16,15],[10,14],[16,27],[15,8],[15,6],[0,13],[20,16],[21,2],[15,6],[24,15],[17,15],[15,24],[22,15],[20,15],[20,15],[15,0],[15,11],[18,13],[11,13],[25,15],[17,15],[15,9],[3,4],[27,15],[15,24],[7,15],[13,9],[15,17],[12,15],[15,4],[29,15],[25,3],[20,15],[15,10],[15,10],[4,3],[8,2],[15,4],[16,0],[13,15],[11,15],[7,27],[17,8],[1,21],[15,17],[23,15],[15,31],[27,6],[15,3],[3,1],[15,4],[14,15],[23,12],[0,2],[15,30],[15,0],[30,15],[15,29],[5,15],[23,12],[28,4],[12,29],[6,4],[15,1],[15,9],[12,15],[18,15],[15,3],[15,10],[9,17],[15,11],[20,15],[15,30],[29,4],[25,15],[15,21],[16,15],[15,26],[15,29],[7,15],[3,15],[15,6],[15,18],[15,16],[18,14],[15,12],[12,7],[28,5],[16,15],[10,15],[15,29],[15,30],[17,23],[2,17],[2,19],[15,2],[7,15],[1,15],[4,1],[15,23],[28,23],[15,3],[25,14],[17,27],[29,15],[8,6],[0,22],[15,12],[20,15],[16,4],[26,15],[1,16],[15,5],[25,0],[19,27],[15,30],[17,1],[5,15],[17,15],[6,18],[21,15],[23,2],[28,9],[0,22],[15,1],[28,15],[31,11],[21,8],[8,16],[2,0],[27,15],[15,20],[23,15],[15,18],[9,17],[6,21],[15,12],[6,28],[12,20],[26,18],[23,17],[3,15],[6,15],[9,15],[30,16],[15,2],[29,9],[21,15],[15,7],[24,27],[6,19],[15,12],[15,29],[16,15],[31,15],[10,15],[15,12],[15,26],[1,15],[15,0],[17,9],[15,21],[29,15],[15,6],[15,9],[15,18],[15,30],[20,15],[15,11],[26,15],[0,15],[15,9],[15,19],[15,22],[15,18],[15,12],[15,28],[15,26],[15,16],[9,12],[15,26],[1,20],[15,13],[15,14],[15,29],[21,15],[15,16],[15,0],[10,22],[23,15],[31,8],[9,13],[3,15],[16,9],[9,27],[15,31],[24,5],[9,15],[15,25],[3,23],[15,9],[31,15],[15,9],[26,18],[15,5],[15,21],[15,19],[15,17],[0,13],[12,15],[0,10],[15,29],[14,21],[0,15],[25,18],[15,9],[7,15],[15,9],[15,17],[1,8],[8,7],[26,23],[27,14],[15,16]],[[1,3],[15,0],[7,9],[12,2],[15,4],[15,7],[15,2],[4,15],[27,4],[10,15],[4,15],[15,14],[15,26],[19,15],[15,1],[15,31],[21,4],[23,31],[15,0],[15,29],[10,2],[20,15],[15,25],[10,17],[15,10],[1,2],[15,30],[5,0],[15,27],[15,1],[13,23],[15,12],[10,15],[15,22],[25,15],[15,6],[29,15],[8,15],[15,23],[22,3],[15,6],[15,24],[25,15],[19,15],[27,5],[17,15],[15,22],[19,15],[29,15],[15,1],[15,2],[18,7],[20,15],[16,21],[16,15],[1,15],[15,28],[31,20],[15,29],[15,13],[15,9],[15,26],[15,3],[10,27],[15,28],[4,15],[15,5],[10,19],[15,21],[2,17],[2,15],[15,24],[9,13],[16,1],[11,26],[3,5],[27,15],[15,6],[29,26],[0,15],[15,20],[15,30],[18,15],[15,17],[31,6],[15,11],[15,28],[30,15],[15,2],[9,15],[7,15],[15,6],[6,15],[15,0],[18,1],[14,15],[13,15],[15,13],[31,16],[15,21],[15,5],[9,15],[15,23],[15,27],[4,28],[18,10],[15,18],[29,25],[0,26],[0,26],[3,15],[24,2],[15,18],[15,3],[26,15],[28,15],[2,3],[28,15],[1,15],[9,15],[15,4],[9,15],[15,22],[5,15],[15,0],[17,15],[15,30],[16,15],[16,14],[7,15],[5,22],[18,15],[15,27],[15,24],[15,22],[30,15],[0,15],[22,10],[15,10],[15,2],[15,23],[27,10],[13,15],[7,12],[15,25],[15,14],[0,15],[15,30],[15,2],[15,1],[30,21],[18,12],[18,15],[15,5],[24,31],[15,27],[15,6],[25,15],[15,10],[15,16],[7,15],[15,23],[16,15],[0,29],[3,27],[15,13],[15,17],[15,17],[15,10],[16,15],[27,15],[4,8],[19,7],[15,10],[15,22],[21,15],[23,0],[0,24],[26,15],[12,15],[11,10],[15,1],[15,21],[15,17],[1,23],[31,26],[16,15],[26,15],[29,6],[15,24],[15,20],[29,30],[2,11],[5,25],[2,17],[15,26],[19,15],[15,12],[23,15],[24,17],[15,22],[15,8],[15,27],[1,15],[4,21],[15,19],[14,19],[15,30],[8,15],[13,15],[15,20],[7,15],[15,30],[6,7],[15,3],[17,8],[15,5],[15,31],[10,15],[9,15],[18,14],[21,4],[15,18],[15,3],[12,5],[15,10],[15,8],[15,5],[15,14],[28,15],[15,26],[15,19],[15,26],[12,15],[26,15],[15,3],[29,15],[15,23],[2,24],[19,18],[17,15],[15,24],[15,2],[7,6],[26,15],[26,23],[15,12],[11,15],[15,24],[30,19],[15,24],[15,20],[21,15],[6,15],[10,15],[15,31]],[[0,15],[0,15],[15,10],[4,15],[10,7],[15,18],[3,15],[7,25],[10,15],[15,26],[2,4],[15,18],[23,9],[15,12],[15,0],[15,25],[19,4],[22,21],[0,10],[15,1],[15,0],[15,24],[15,7],[0,27],[7,30],[15,29],[1,15],[15,10],[3,31],[15,27],[23,12],[9,15],[18,10],[15,0],[19,0],[15,20],[7,29],[17,15],[28,23],[15,19],[23,13],[3,15],[1,15],[17,20],[1,26],[15,19],[27,15],[16,15],[15,2],[5,27],[30,8],[25,27],[16,15],[15,20],[20,14],[15,25],[10,12],[15,6],[15,21],[15,0],[15,26],[16,15],[7,2],[21,2],[15,14],[15,18],[18,15],[15,6],[12,15],[15,2],[7,26],[15,21],[15,28],[22,27],[15,23],[3,15],[15,27],[15,21],[3,15],[15,1],[15,16],[21,20],[15,28],[15,0],[16,23],[15,27],[25,16],[19,15],[15,22],[15,6],[30,15],[15,26],[15,30],[19,16],[15,23],[15,1],[8,3],[16,15],[31,15],[19,23],[24,20],[0,5],[16,25],[15,3],[3,21],[15,24],[15,3],[15,14],[26,15],[15,21],[15,22],[15,31],[25,15],[22,15],[15,21],[11,21],[15,12],[13,15],[24,5],[8,26],[6,19],[31,20],[0,9],[15,24],[15,2],[13,25],[2,15],[2,5],[14,15],[15,5],[15,14],[0,27],[15,7],[31,15],[15,8],[10,15],[15,24],[15,25],[4,15],[23,15],[22,12],[15,8],[15,14],[4,15],[6,15],[13,15],[15,4],[15,17],[11,10],[22,1],[21,4],[16,4],[15,30],[31,9],[5,17],[7,17],[15,23],[13,15],[15,8],[19,7],[25,15],[15,4],[15,1],[16,15],[14,15],[15,12],[18,15],[5,15],[4,15],[15,25],[15,22],[21,19],[10,8],[18,15],[15,29],[27,15],[15,8],[15,3],[15,25],[15,31],[15,18],[15,29],[15,2],[15,26],[7,27],[14,15],[28,24],[15,24],[21,5],[26,14],[15,22],[2,15],[15,4],[2,15],[15,4],[4,15],[15,7],[31,27],[6,24],[8,5],[11,15],[15,14],[6,26],[15,6],[15,10],[6,27],[27,15],[4,15],[4,15],[15,22],[24,31],[8,26],[6,4],[17,15],[30,10],[1,15],[14,12],[15,3],[15,29],[2,6],[8,15],[15,24],[8,27],[15,16],[30,15],[15,8],[15,24],[15,28],[11,17],[4,15],[29,15],[0,15],[1,22],[22,11],[20,15],[15,6],[28,20],[15,1],[0,18],[30,15],[15,17],[15,29],[6,30],[4,20],[15,11],[15,22],[13,15],[3,15],[24,15],[15,11],[30,15],[15,18],[0,15],[15,1],[15,7],[9,15]],[[15,3],[3,23],[24,17],[17,15],[15,26],[23,8],[30,15],[16,1],[19,13],[11,14],[16,15],[14,5],[12,15],[20,28],[29,15],[0,15],[22,20],[27,15],[28,15],[19,15],[9,15],[15,5],[0,27],[3,7],[15,31],[0,29],[0,13],[27,12],[15,0],[15,31],[15,7],[2,28],[27,15],[15,2],[2,22],[20,7],[4,15],[15,13],[19,26],[13,15],[15,28],[1,31],[12,9],[15,18],[15,9],[8,22],[15,18],[14,15],[28,2],[22,17],[1,15],[15,3],[15,25],[30,28],[15,5],[15,20],[7,13],[15,1],[15,23],[23,15],[17,14],[15,16],[31,1],[9,8],[3,8],[23,2],[15,30],[15,22],[15,18],[29,15],[15,20],[15,8],[19,15],[15,25],[15,9],[15,6],[15,14],[24,0],[15,6],[18,8],[7,17],[11,27],[3,15],[15,23],[15,1],[15,10],[20,15],[25,15],[7,15],[4,7],[9,0],[20,15],[15,16],[15,30],[20,21],[15,17],[15,25],[15,6],[23,15],[31,15],[16,23],[27,8],[22,27],[18,10],[15,17],[20,3],[26,15],[20,10],[2,15],[15,30],[15,17],[15,22],[15,17],[15,4],[15,11],[15,14],[15,14],[15,29],[16,15],[6,15],[15,21],[24,4],[15,22],[24,15],[15,11],[4,15],[1,11],[26,25],[2,5],[15,12],[19,22],[23,15],[26,15],[3,15],[15,2],[15,10],[15,22],[15,8],[15,28],[1,25],[1,21],[15,17],[22,6],[7,15],[26,5],[2,15],[15,22],[18,1],[15,17],[11,15],[0,20],[25,31],[19,24],[26,17],[15,29],[15,31],[15,17],[31,1],[15,5],[2,15],[11,27],[15,1],[15,11],[15,9],[15,13],[9,29],[15,14],[15,16],[25,2],[15,4],[15,14],[6,15],[20,26],[22,4],[15,30],[15,31],[15,17],[22,15],[12,15],[28,15],[16,15],[4,3],[15,25],[9,22],[12,28],[15,27],[15,31],[26,5],[5,28],[14,15],[8,3],[15,22],[11,15],[9,13],[15,13],[15,19],[19,28],[14,15],[22,20],[20,10],[29,15],[15,21],[15,21],[15,8],[5,15],[15,6],[27,15],[28,0],[15,6],[7,20],[15,16],[31,17],[17,2],[29,15],[6,15],[15,23],[6,14],[2,15],[30,15],[30,15],[1,16],[21,15],[9,15],[3,27],[15,2],[15,6],[19,21],[21,15],[16,15],[15,17],[15,14],[15,6],[15,29],[18,15],[6,15],[6,27],[15,7],[7,14],[15,18],[19,16],[26,20],[15,16],[23,29],[30,15],[19,15],[15,12],[15,2],[15,18],[22,15],[0,21],[15,26],[31,21],[15,29],[7,15],[15,25],[11,15]],[[20,18],[31,15],[29,22],[15,31],[14,12],[17,20],[16,1],[15,8],[15,17],[3,1],[16,18],[24,15],[19,30],[8,2],[0,30],[30,15],[2,15],[16,15],[15,27],[15,4],[15,26],[15,21],[15,6],[10,1],[15,1],[15,16],[15,5],[15,24],[15,19],[15,31],[15,29],[5,27],[19,18],[15,24],[15,28],[4,15],[25,22],[21,15],[15,30],[22,23],[15,28],[20,14],[15,16],[5,15],[15,1],[13,15],[15,25],[15,25],[30,6],[16,24],[15,1],[15,27],[4,28],[2,6],[13,0],[15,31],[17,15],[10,4],[31,12],[15,7],[15,1],[15,28],[7,15],[15,20],[15,28],[4,15],[11,12],[13,23],[4,15],[11,13],[4,15],[26,31],[21,8],[15,11],[3,15],[7,15],[17,4],[5,29],[15,11],[15,3],[29,25],[29,15],[25,15],[15,5],[15,17],[12,13],[10,15],[19,24],[15,22],[15,8],[10,12],[15,11],[4,15],[15,11],[21,15],[8,15],[23,25],[27,15],[15,30],[15,13],[15,1],[7,29],[0,15],[8,15],[25,3],[10,15],[13,18],[29,30],[15,2],[15,8],[26,15],[15,19],[17,4],[14,22],[24,14],[11,15],[11,6],[5,15],[15,24],[15,25],[7,20],[15,14],[4,15],[4,9],[27,15],[30,27],[6,15],[15,12],[15,30],[16,12],[20,6],[7,2],[7,15],[16,19],[15,2],[12,15],[29,31],[22,9],[24,15],[25,15],[30,14],[15,5],[15,29],[19,22],[15,20],[15,31],[15,27],[15,17],[27,9],[15,5],[15,11],[18,15],[8,29],[15,0],[13,15],[15,22],[15,12],[15,23],[31,4],[15,31],[4,30],[4,0],[8,15],[29,11],[19,21],[7,15],[15,21],[6,15],[2,5],[26,21],[5,15],[15,18],[24,14],[13,26],[18,4],[16,15],[31,15],[2,4],[15,29],[15,5],[5,15],[15,10],[15,24],[17,29],[22,7],[23,15],[18,15],[29,15],[28,15],[19,15],[3,15],[21,28],[2,15],[15,16],[15,8],[15,6],[15,16],[15,20],[15,20],[15,18],[27,15],[15,21],[18,27],[12,31],[15,19],[22,15],[26,15],[3,15],[15,17],[15,4],[20,30],[28,16],[3,26],[7,6],[28,26],[5,15],[8,29],[15,1],[1,15],[3,15],[5,8],[15,5],[27,24],[15,23],[0,6],[13,20],[15,11],[15,11],[15,4],[5,15],[8,28],[10,15],[15,30],[15,5],[31,15],[17,3],[5,19],[15,31],[15,31],[21,15],[20,29],[15,11],[15,8],[15,10],[15,7],[6,15],[15,29],[25,15],[15,1],[15,9],[9,24],[15,14],[5,15],[15,18],[19,15],[15,12]],[[28,15],[5,9],[1,12],[15,21],[1,26],[29,15],[15,21],[21,15],[15,7],[25,15],[4,16],[2,23],[15,20],[22,13],[15,22],[20,23],[19,31],[15,16],[15,6],[15,30],[28,15],[15,1],[0,21],[15,10],[15,9],[10,18],[30,15],[15,19],[21,15],[15,3],[26,11],[28,15],[15,24],[15,0],[20,8],[15,5],[31,13],[24,23],[15,4],[16,26],[15,4],[13,29],[23,15],[6,3],[15,1],[15,10],[15,31],[8,15],[15,27],[15,9],[15,18],[8,15],[10,15],[15,10],[28,21],[15,4],[15,20],[15,10],[6,15],[20,15],[17,22],[7,15],[15,27],[15,10],[15,3],[15,19],[22,15],[0,27],[15,20],[15,3],[2,16],[15,16],[15,30],[3,26],[15,3],[15,13],[15,14],[2,21],[15,18],[15,22],[15,10],[28,15],[15,22],[1,15],[11,18],[15,16],[31,15],[15,10],[16,15],[15,2],[15,3],[15,4],[31,9],[15,27],[0,19],[25,15],[14,15],[15,17],[7,6],[15,7],[18,25],[21,7],[22,6],[15,30],[17,15],[15,20],[15,20],[31,5],[8,20],[9,15],[22,15],[15,13],[28,11],[26,15],[23,15],[15,16],[15,17],[25,22],[11,15],[15,29],[15,5],[7,15],[11,15],[27,15],[15,18],[17,24],[28,5],[15,8],[15,26],[1,23],[15,7],[4,20],[16,15],[2,15],[15,18],[2,15],[16,31],[15,27],[19,15],[28,4],[15,9],[25,15],[18,4],[22,15],[15,29],[15,29],[28,15],[15,30],[15,28],[17,1],[28,7],[29,7],[15,14],[12,15],[15,8],[24,31],[18,15],[15,2],[30,2],[12,15],[15,17],[15,29],[8,15],[15,23],[15,16],[12,30],[15,31],[8,15],[15,28],[15,12],[16,1],[6,15],[27,23],[15,13],[7,30],[11,19],[18,10],[15,5],[24,15],[16,26],[3,15],[15,10],[2,15],[15,3],[30,21],[6,21],[15,10],[29,22],[22,28],[6,15],[27,10],[26,15],[16,5],[15,30],[15,8],[16,5],[15,2],[2,15],[4,15],[15,29],[29,15],[15,29],[29,12],[15,17],[15,31],[15,23],[15,14],[15,24],[4,11],[15,10],[3,15],[14,29],[25,15],[1,15],[15,27],[15,13],[29,15],[29,15],[16,15],[3,15],[25,21],[15,17],[15,25],[28,26],[26,0],[15,5],[16,1],[15,30],[16,20],[15,27],[15,12],[20,11],[9,15],[14,5],[15,19],[26,21],[15,21],[15,6],[26,15],[15,28],[30,15],[15,3],[21,15],[0,10],[24,15],[10,20],[2,29],[15,17],[4,15],[4,7],[15,18],[5,15],[29,9],[15,24],[8,26],[5,2]],[[29,15],[21,26],[15,26],[5,14],[23,15],[15,6],[15,21],[17,15],[28,31],[15,25],[2,15],[15,17],[15,0],[14,15],[15,24],[19,15],[15,21],[15,27],[22,15],[15,9],[3,15],[15,23],[11,20],[7,3],[3,15],[30,15],[0,15],[1,23],[4,30],[28,15],[16,27],[15,10],[15,24],[11,15],[15,2],[15,5],[15,13],[22,23],[13,12],[0,15],[20,8],[15,4],[23,15],[15,13],[17,15],[23,15],[29,19],[15,6],[15,25],[23,15],[20,15],[15,2],[15,11],[15,25],[7,24],[15,20],[5,15],[15,19],[15,25],[15,26],[15,14],[15,8],[15,11],[24,15],[10,15],[18,0],[15,17],[31,15],[19,8],[5,15],[19,15],[15,18],[26,8],[19,11],[13,29],[15,16],[15,25],[22,19],[9,13],[13,1],[15,19],[15,5],[27,15],[10,18],[15,30],[15,30],[14,15],[7,15],[15,4],[16,23],[30,15],[15,2],[14,15],[15,12],[15,27],[15,7],[15,10],[17,27],[15,8],[7,15],[17,25],[15,9],[15,2],[15,4],[1,15],[12,15],[15,10],[15,27],[15,18],[15,11],[29,15],[15,6],[15,29],[15,2],[10,1],[11,15],[15,19],[5,3],[7,11],[10,15],[11,15],[15,16],[15,30],[27,24],[8,15],[15,13],[15,0],[17,15],[15,12],[15,23],[12,15],[15,19],[2,19],[29,23],[15,25],[15,3],[15,22],[15,9],[15,18],[21,15],[26,5],[15,24],[15,27],[20,15],[24,27],[15,12],[11,15],[27,20],[21,12],[15,27],[27,30],[15,22],[15,28],[20,15],[16,15],[15,9],[15,25],[30,15],[15,23],[15,25],[9,6],[17,5],[15,6],[25,28],[15,27],[11,15],[23,24],[13,15],[12,27],[15,0],[6,15],[14,15],[0,21],[15,14],[15,10],[1,15],[15,2],[31,21],[31,10],[21,15],[15,2],[3,8],[12,15],[15,18],[15,9],[3,5],[12,23],[8,19],[15,7],[8,15],[29,7],[18,15],[15,23],[30,15],[20,27],[4,18],[8,18],[15,26],[15,23],[15,29],[30,26],[15,0],[16,29],[15,22],[15,7],[1,8],[15,27],[15,5],[15,27],[14,8],[15,30],[25,6],[15,4],[15,30],[6,16],[3,17],[15,22],[4,15],[25,15],[15,16],[15,25],[22,20],[0,29],[26,25],[24,26],[4,26],[15,23],[15,29],[15,10],[15,2],[15,12],[30,15],[5,15],[15,12],[8,9],[15,17],[29,15],[0,15],[29,15],[3,14],[15,13],[13,24],[3,19],[6,0],[7,5],[22,17],[6,15],[15,23],[2,15],[21,15],[15,31],[17,15],[15,31],[6,7],[27,10],[4,15]],[[15,11],[14,15],[30,3],[15,18],[12,23],[15,29],[15,27],[28,27],[15,6],[2,16],[15,23],[15,2],[15,10],[15,3],[15,14],[8,15],[9,15],[15,30],[26,27],[20,8],[2,7],[15,14],[15,17],[15,21],[10,15],[31,15],[9,5],[15,20],[24,22],[20,15],[15,9],[15,17],[9,17],[10,9],[5,29],[15,8],[0,2],[15,31],[6,15],[2,21],[10,25],[3,15],[15,7],[8,15],[23,5],[0,15],[13,26],[15,6],[15,30],[4,15],[15,9],[15,26],[3,11],[15,24],[14,15],[15,23],[15,9],[6,25],[15,14],[15,1],[5,15],[16,0],[15,0],[13,1],[15,20],[22,15],[11,15],[23,15],[27,11],[4,23],[7,17],[15,31],[4,1],[22,27],[15,7],[31,12],[13,16],[6,3],[15,24],[4,5],[15,14],[25,15],[4,15],[15,6],[15,5],[26,15],[15,20],[23,20],[7,15],[10,15],[11,5],[15,12],[15,11],[29,3],[17,12],[15,31],[15,12],[24,13],[15,5],[15,6],[21,31],[5,12],[9,25],[15,19],[2,15],[15,21],[15,12],[1,15],[15,17],[23,8],[19,15],[23,15],[3,18],[31,15],[1,15],[15,25],[17,15],[19,5],[23,15],[4,21],[15,28],[15,4],[15,27],[12,5],[7,25],[17,7],[15,31],[13,15],[8,22],[27,15],[18,9],[15,12],[7,15],[24,9],[11,26],[15,10],[15,24],[18,15],[28,15],[15,2],[15,28],[15,12],[2,15],[29,26],[20,22],[15,27],[1,5],[31,16],[15,1],[7,8],[11,15],[16,19],[1,25],[15,21],[15,9],[15,3],[15,13],[10,15],[27,15],[15,14],[6,15],[15,9],[14,23],[9,15],[3,12],[15,18],[9,27],[3,15],[15,24],[1,15],[15,5],[23,15],[24,15],[15,31],[17,11],[12,15],[15,30],[15,11],[30,14],[24,29],[31,21],[15,8],[26,15],[7,6],[30,4],[16,24],[15,5],[23,11],[2,15],[0,4],[0,15],[17,25],[11,15],[15,6],[15,19],[26,14],[15,1],[15,24],[15,6],[17,21],[6,20],[4,31],[1,29],[15,29],[19,28],[15,18],[0,14],[15,29],[22,24],[22,15],[15,13],[17,15],[14,23],[24,23],[15,7],[1,0],[15,4],[15,8],[15,3],[15,4],[9,15],[15,21],[26,6],[25,12],[4,23],[4,15],[3,16],[15,19],[25,26],[15,17],[0,15],[28,6],[21,20],[31,24],[16,15],[4,15],[1,4],[26,16],[22,15],[6,15],[22,31],[6,11],[15,21],[15,30],[9,15],[15,7],[15,0],[15,12],[10,15],[15,16],[30,15],[15,7],[20,15],[29,5],[15,16],[15,0]],[[5,15],[16,31],[9,25],[13,30],[21,30],[0,30],[23,26],[15,23],[15,20],[0,15],[18,26],[15,29],[23,15],[24,5],[15,11],[15,4],[15,0],[15,9],[15,8],[26,30],[22,18],[3,25],[19,7],[15,14],[15,11],[15,8],[15,13],[12,11],[15,14],[15,4],[14,15],[2,15],[15,0],[8,15],[8,15],[13,1],[12,15],[31,14],[17,11],[15,20],[21,17],[18,15],[15,18],[9,15],[31,15],[1,23],[15,12],[15,20],[15,14],[16,15],[29,15],[15,5],[11,15],[15,12],[8,7],[15,0],[15,1],[19,18],[16,27],[15,31],[15,5],[15,7],[1,25],[30,15],[26,5],[5,31],[15,7],[12,15],[15,5],[15,23],[14,31],[11,4],[4,21],[31,14],[9,6],[26,15],[22,31],[30,19],[25,15],[15,18],[27,25],[15,16],[19,15],[15,25],[15,21],[15,5],[15,30],[18,19],[15,13],[23,15],[21,15],[2,28],[17,5],[7,15],[15,9],[15,11],[1,5],[15,27],[18,15],[15,18],[15,26],[13,19],[14,15],[7,15],[26,4],[15,20],[15,13],[4,30],[18,6],[15,5],[15,22],[9,16],[18,15],[26,20],[9,15],[28,3],[15,23],[30,27],[0,30],[25,17],[15,19],[12,9],[23,15],[15,6],[20,15],[30,15],[15,20],[16,24],[15,26],[3,17],[30,0],[15,0],[15,19],[16,15],[15,9],[15,6],[9,15],[15,7],[15,20],[6,15],[0,15],[14,15],[15,27],[23,31],[15,22],[20,15],[9,15],[8,29],[26,10],[9,15],[4,15],[6,17],[23,15],[4,15],[6,12],[15,22],[24,15],[15,31],[15,7],[10,30],[11,29],[15,23],[25,15],[15,11],[15,7],[15,3],[2,11],[0,7],[13,15],[1,15],[9,13],[15,3],[15,23],[11,15],[3,15],[20,8],[15,30],[23,15],[12,15],[12,15],[1,15],[15,4],[26,16],[25,15],[23,3],[14,13],[15,10],[15,7],[30,15],[5,15],[20,16],[15,20],[24,15],[13,15],[29,15],[15,18],[22,4],[24,22],[11,15],[15,10],[15,0],[23,6],[6,15],[15,27],[15,25],[15,27],[15,1],[25,18],[28,18],[15,26],[4,1],[3,15],[15,10],[3,4],[16,8],[12,8],[6,4],[15,5],[15,20],[21,10],[15,13],[15,0],[14,15],[15,7],[16,14],[13,15],[14,16],[4,31],[15,14],[8,15],[15,9],[9,15],[15,25],[7,9],[15,23],[2,21],[15,19],[3,14],[15,24],[7,23],[4,0],[0,30],[15,3],[13,30],[15,21],[15,26],[18,15],[15,8],[22,15],[11,15],[14,23],[15,1],[15,16],[15,29],[15,20],[26,15]],[[15,29],[15,22],[4,27],[21,15],[15,2],[13,9],[15,22],[15,21],[21,8],[3,15],[15,14],[12,15],[29,23],[15,6],[15,1],[15,6],[15,9],[15,22],[2,17],[30,15],[15,30],[15,24],[6,24],[15,31],[19,27],[15,22],[10,15],[24,15],[15,25],[2,22],[25,23],[17,5],[28,30],[9,15],[0,15],[15,24],[15,16],[15,23],[8,14],[15,11],[23,15],[20,15],[16,5],[11,4],[11,3],[15,3],[10,31],[15,17],[13,15],[15,21],[12,15],[12,27],[23,15],[15,19],[3,15],[27,15],[15,9],[29,1],[15,23],[15,2],[15,24],[15,27],[15,10],[3,31],[15,30],[10,15],[23,15],[15,24],[21,20],[27,15],[15,30],[15,19],[15,9],[18,15],[15,14],[4,15],[13,15],[24,15],[6,15],[16,15],[15,26],[20,28],[15,31],[6,3],[15,4],[15,4],[1,12],[27,8],[7,17],[6,31],[15,28],[15,3],[17,9],[2,23],[15,17],[27,15],[18,7],[6,14],[15,19],[13,27],[29,11],[10,15],[20,15],[9,15],[15,7],[13,1],[15,8],[20,14],[7,15],[30,7],[22,19],[15,30],[31,4],[15,1],[15,9],[15,29],[1,11],[21,16],[15,24],[12,15],[16,6],[15,2],[5,1],[15,6],[11,15],[0,15],[15,7],[8,24],[30,28],[12,10],[20,19],[5,15],[15,13],[15,1],[23,15],[15,2],[28,8],[15,19],[7,12],[17,28],[15,10],[0,15],[15,22],[15,18],[12,1],[17,15],[6,13],[15,14],[22,14],[20,23],[15,10],[15,22],[28,15],[15,27],[15,9],[15,8],[15,5],[4,15],[23,15],[15,13],[8,28],[18,15],[8,2],[15,5],[29,15],[15,27],[15,10],[0,31],[0,15],[2,31],[15,18],[20,3],[31,9],[12,14],[15,3],[15,23],[29,15],[15,17],[15,29],[19,15],[15,12],[15,4],[15,1],[15,10],[8,13],[7,15],[15,5],[15,29],[28,6],[19,15],[25,15],[15,11],[8,14],[30,25],[22,15],[19,15],[14,28],[15,23],[27,15],[15,0],[15,6],[23,9],[2,5],[18,12],[15,4],[15,31],[17,15],[13,14],[11,15],[27,26],[15,28],[15,4],[9,19],[15,5],[15,20],[15,7],[10,2],[23,7],[15,2],[5,15],[18,15],[1,16],[19,15],[22,28],[14,21],[15,23],[15,23],[15,4],[15,16],[15,18],[3,23],[21,6],[8,15],[30,10],[15,6],[14,15],[3,15],[15,18],[15,14],[15,7],[22,15],[11,29],[15,18],[15,26],[26,15],[3,14],[9,15],[15,21],[20,25],[15,9],[4,15],[15,21],[27,15],[2,24],[15,31],[15,7]],[[15,2],[20,17],[15,0],[15,9],[15,24],[17,15],[15,30],[8,10],[4,15],[13,24],[15,24],[30,15],[15,16],[15,22],[8,23],[4,15],[20,24],[9,29],[14,30],[15,6],[11,0],[30,29],[14,15],[15,7],[10,23],[11,15],[15,11],[15,31],[10,15],[15,13],[15,4],[15,10],[15,25],[2,1],[24,15],[30,13],[5,15],[28,15],[2,15],[15,3],[15,3],[2,15],[15,6],[15,10],[15,7],[4,19],[15,7],[15,25],[9,5],[9,11],[9,13],[25,31],[15,28],[15,22],[13,27],[15,29],[15,9],[6,15],[15,24],[5,18],[15,1],[15,0],[27,19],[0,15],[15,10],[15,11],[3,28],[15,21],[24,15],[31,15],[19,26],[3,15],[15,12],[15,18],[15,12],[9,11],[15,8],[17,15],[20,13],[15,29],[20,6],[0,21],[1,30],[15,24],[23,15],[15,7],[11,15],[1,15],[15,31],[10,28],[4,24],[25,5],[31,25],[15,19],[15,12],[20,15],[15,23],[25,16],[15,24],[6,11],[15,14],[15,3],[8,15],[15,0],[30,15],[12,20],[7,26],[15,13],[15,21],[17,15],[15,31],[15,9],[10,30],[15,17],[15,8],[15,19],[24,15],[15,1],[18,22],[2,24],[15,5],[15,9],[2,11],[6,24],[20,17],[10,31],[15,5],[16,15],[22,2],[15,11],[24,15],[5,18],[18,7],[15,31],[7,14],[7,5],[12,3],[15,14],[2,28],[6,18],[15,13],[5,21],[27,12],[12,15],[15,8],[15,11],[5,2],[15,25],[19,23],[23,5],[10,6],[22,21],[15,28],[15,12],[15,19],[16,5],[30,15],[3,31],[15,21],[24,13],[15,27],[15,20],[16,15],[15,2],[20,26],[15,8],[15,4],[23,10],[15,26],[30,21],[15,23],[9,7],[15,13],[15,2],[15,20],[14,2],[9,12],[15,28],[15,7],[20,15],[15,25],[15,30],[15,25],[31,15],[15,7],[15,7],[15,27],[15,22],[19,15],[17,26],[15,21],[13,0],[15,21],[5,27],[15,8],[12,15],[15,14],[4,24],[20,15],[14,15],[7,28],[16,15],[15,13],[15,10],[26,16],[5,15],[3,25],[3,15],[15,16],[1,15],[15,19],[16,13],[1,15],[15,8],[9,26],[15,9],[20,15],[15,5],[15,24],[15,31],[23,25],[15,30],[25,17],[23,15],[15,1],[2,15],[10,15],[15,31],[19,3],[19,7],[21,18],[15,5],[11,28],[15,0],[15,23],[15,19],[29,12],[22,15],[2,15],[15,12],[6,9],[29,15],[15,13],[15,24],[15,20],[15,10],[29,7],[8,7],[17,13],[15,26],[23,14],[15,21],[10,13],[4,15],[15,8],[15,28]],[[4,15],[22,15],[15,16],[15,6],[2,5],[21,18],[7,18],[8,31],[27,15],[15,16],[15,14],[13,11],[12,21],[16,6],[0,15],[24,15],[19,15],[16,17],[30,22],[15,19],[26,3],[18,13],[15,17],[15,11],[19,13],[15,20],[4,1],[15,6],[20,14],[2,16],[15,31],[15,28],[15,5],[8,27],[10,15],[24,15],[6,15],[15,11],[24,15],[15,8],[9,15],[8,9],[8,29],[30,22],[3,10],[29,0],[2,15],[21,9],[19,15],[15,28],[26,2],[17,10],[22,25],[28,23],[15,27],[15,16],[22,29],[15,3],[11,15],[3,15],[13,15],[15,24],[12,15],[15,4],[23,15],[15,13],[31,13],[23,30],[8,5],[15,19],[6,17],[15,29],[22,15],[15,17],[25,16],[15,28],[15,20],[8,4],[15,2],[19,15],[31,22],[22,15],[12,27],[23,15],[15,0],[15,25],[15,23],[15,21],[15,25],[13,7],[9,27],[15,29],[15,5],[21,15],[15,2],[28,7],[21,4],[11,15],[15,30],[24,15],[15,31],[9,27],[29,15],[15,17],[12,24],[15,21],[15,14],[8,15],[15,20],[8,31],[15,19],[26,15],[31,22],[0,15],[24,22],[20,15],[8,15],[26,20],[8,28],[15,16],[15,18],[15,8],[14,0],[15,11],[26,15],[8,14],[19,15],[16,15],[22,15],[15,21],[5,15],[0,15],[17,16],[15,31],[15,16],[15,7],[27,25],[28,26],[8,10],[15,20],[2,15],[16,19],[17,19],[15,10],[17,1],[15,3],[15,0],[0,13],[10,18],[23,15],[15,13],[23,24],[15,7],[15,7],[2,4],[0,15],[15,17],[15,21],[15,3],[16,14],[15,5],[17,15],[4,30],[15,1],[11,14],[15,9],[10,29],[15,21],[1,5],[0,9],[21,20],[23,4],[27,9],[15,19],[13,15],[15,5],[11,13],[1,13],[31,15],[10,15],[15,25],[4,15],[15,4],[15,14],[15,9],[0,15],[18,19],[30,4],[15,30],[15,6],[30,1],[15,0],[15,31],[15,22],[23,11],[15,19],[15,22],[7,15],[11,15],[21,15],[16,0],[5,14],[30,15],[1,15],[15,1],[15,11],[15,25],[9,15],[15,24],[15,7],[22,15],[11,25],[15,1],[15,23],[15,1],[8,15],[8,14],[22,11],[15,25],[27,15],[15,28],[15,16],[15,22],[7,21],[11,17],[18,11],[11,31],[9,16],[15,6],[15,20],[15,14],[15,16],[15,0],[15,1],[9,15],[19,15],[10,27],[15,17],[3,15],[14,2],[15,14],[15,16],[25,7],[15,25],[15,9],[10,15],[12,27],[23,16],[23,15],[15,26],[2,15],[14,8],[7,24],[14,9],[17,30],[25,30]],[[15,21],[20,8],[15,19],[2,8],[15,20],[6,17],[8,19],[15,3],[15,22],[4,9],[20,4],[25,10],[15,20],[15,19],[15,6],[27,15],[15,1],[4,15],[15,20],[8,7],[4,16],[15,24],[15,2],[15,5],[4,15],[15,24],[15,3],[16,27],[13,4],[15,16],[22,15],[15,9],[15,23],[17,15],[2,22],[15,22],[21,15],[0,16],[15,9],[10,15],[15,13],[28,4],[15,12],[15,22],[15,2],[13,29],[15,12],[8,22],[15,29],[15,16],[15,1],[15,27],[15,10],[15,7],[15,24],[17,15],[15,13],[25,15],[15,22],[15,30],[2,15],[27,15],[15,24],[15,21],[11,1],[6,12],[15,17],[15,20],[15,14],[15,29],[9,11],[15,7],[6,15],[2,10],[15,21],[27,15],[23,3],[15,16],[15,23],[15,1],[4,15],[27,15],[31,11],[5,7],[2,15],[31,0],[15,0],[15,9],[15,27],[29,27],[27,15],[27,0],[24,15],[30,15],[15,1],[25,5],[15,19],[30,15],[15,4],[14,15],[21,15],[15,31],[15,25],[15,13],[31,6],[29,8],[23,15],[30,13],[24,2],[4,15],[15,12],[29,15],[24,19],[15,1],[8,25],[8,15],[7,15],[14,18],[15,21],[15,28],[6,15],[26,15],[22,25],[15,18],[28,15],[1,15],[15,31],[4,29],[15,4],[15,31],[15,30],[15,2],[16,2],[15,12],[21,0],[15,18],[28,15],[15,5],[18,9],[15,6],[15,6],[6,9],[15,19],[27,14],[15,13],[15,30],[16,18],[9,1],[22,12],[15,12],[16,15],[15,30],[15,23],[3,15],[31,15],[22,15],[5,30],[15,29],[15,5],[10,6],[15,0],[9,16],[19,14],[15,22],[25,15],[15,24],[3,4],[8,15],[3,15],[5,15],[31,13],[2,15],[15,30],[15,19],[15,7],[15,26],[31,2],[31,23],[11,26],[24,15],[15,28],[0,31],[17,2],[21,8],[15,18],[3,24],[11,15],[0,15],[23,15],[14,1],[15,27],[15,14],[8,2],[0,15],[21,15],[15,20],[3,15],[15,26],[8,15],[11,15],[15,1],[28,31],[15,0],[15,22],[28,27],[15,1],[2,8],[23,17],[13,15],[6,28],[12,15],[15,22],[17,15],[11,28],[12,15],[14,5],[24,7],[5,17],[15,0],[9,25],[15,18],[13,15],[18,12],[9,15],[15,27],[26,7],[15,8],[19,18],[26,15],[17,0],[15,12],[27,29],[15,9],[2,28],[15,9],[10,17],[2,9],[31,15],[15,16],[13,15],[15,14],[15,10],[15,29],[15,11],[15,28],[20,15],[15,11],[2,15],[15,3],[28,15],[12,9],[15,30],[15,24],[15,29],[4,15],[20,16]],[[18,3],[13,15],[3,22],[15,29],[30,15],[15,27],[15,16],[11,31],[15,25],[15,29],[23,15],[15,19],[2,19],[1,19],[30,8],[5,25],[16,25],[1,15],[15,29],[15,1],[3,24],[21,28],[7,12],[15,12],[15,22],[15,4],[28,15],[29,15],[15,0],[23,4],[9,23],[4,15],[26,15],[15,23],[15,7],[15,29],[3,15],[0,10],[13,15],[15,3],[13,8],[24,15],[16,15],[30,21],[15,19],[14,15],[15,27],[15,31],[15,30],[0,15],[15,3],[14,15],[15,5],[28,15],[7,23],[4,31],[3,15],[15,0],[1,12],[5,14],[15,10],[15,20],[13,26],[15,19],[14,15],[27,15],[7,15],[15,12],[15,8],[18,27],[15,18],[15,27],[15,16],[15,21],[4,3],[15,27],[9,24],[1,15],[18,24],[18,15],[7,12],[4,15],[15,19],[15,11],[15,14],[26,22],[15,11],[10,25],[3,15],[15,7],[17,15],[15,3],[15,1],[26,22],[15,24],[27,1],[15,6],[20,15],[4,15],[8,2],[18,0],[15,13],[15,29],[27,15],[29,17],[15,24],[31,28],[15,4],[12,23],[14,15],[13,21],[11,29],[15,26],[24,26],[9,15],[27,15],[7,9],[15,10],[26,15],[15,1],[8,2],[8,15],[15,31],[5,15],[1,23],[15,22],[2,15],[15,3],[0,15],[22,15],[5,28],[15,23],[15,25],[28,15],[15,24],[10,16],[12,15],[15,16],[23,6],[2,16],[15,3],[2,15],[16,9],[28,15],[15,30],[15,9],[8,4],[16,21],[5,28],[15,17],[26,15],[15,21],[15,26],[30,29],[15,5],[8,5],[8,22],[13,10],[15,6],[15,14],[27,15],[24,5],[15,24],[0,15],[27,15],[15,26],[15,28],[15,8],[7,30],[15,11],[20,23],[15,2],[15,23],[7,15],[4,11],[5,15],[6,15],[4,27],[27,13],[15,1],[19,30],[4,24],[8,15],[15,29],[15,9],[29,15],[25,27],[15,4],[15,31],[24,29],[28,15],[8,11],[15,3],[15,30],[8,29],[17,19],[27,17],[15,3],[15,27],[19,5],[16,15],[15,0],[21,15],[12,15],[15,21],[21,19],[15,11],[15,20],[17,29],[15,19],[15,17],[28,13],[24,15],[3,20],[18,10],[9,15],[15,31],[7,18],[2,19],[14,21],[22,1],[15,8],[26,17],[18,15],[15,26],[24,1],[15,9],[15,20],[15,6],[21,17],[30,15],[25,15],[10,0],[15,14],[9,15],[26,15],[21,15],[15,26],[25,20],[13,2],[14,17],[15,0],[28,15],[15,19],[15,3],[15,31],[20,8],[5,15],[9,15],[10,8],[16,25],[2,15],[10,15],[15,28],[3,15],[15,22]],[[10,2],[15,5],[2,15],[15,14],[14,27],[27,15],[9,4],[15,20],[13,3],[15,21],[3,15],[28,14],[15,0],[6,22],[4,3],[11,2],[15,26],[27,15],[12,15],[15,26],[15,11],[6,18],[27,13],[15,2],[15,20],[15,24],[9,26],[3,15],[15,18],[15,7],[28,7],[15,26],[25,15],[0,30],[4,17],[0,15],[15,1],[26,11],[15,6],[4,15],[15,28],[15,13],[17,13],[20,15],[0,17],[15,28],[15,20],[14,20],[15,29],[15,18],[15,0],[22,15],[15,13],[18,15],[26,0],[15,11],[15,22],[15,3],[31,29],[29,15],[14,16],[17,15],[26,15],[16,2],[29,19],[16,15],[13,15],[15,1],[14,15],[15,4],[19,31],[11,15],[5,25],[26,20],[20,26],[15,8],[15,8],[9,15],[6,27],[17,13],[29,15],[29,15],[15,14],[31,15],[15,28],[30,31],[15,30],[9,15],[15,16],[21,18],[22,24],[8,18],[8,15],[15,20],[6,15],[31,0],[15,25],[18,8],[15,8],[15,31],[15,18],[15,31],[26,15],[15,29],[15,29],[28,15],[16,15],[15,14],[15,7],[15,23],[15,25],[21,1],[15,25],[9,15],[16,0],[15,22],[15,20],[22,15],[18,20],[15,12],[13,15],[23,31],[8,15],[31,15],[15,4],[15,22],[15,28],[15,3],[0,15],[28,15],[15,30],[15,9],[5,29],[16,17],[15,7],[0,28],[0,19],[15,9],[23,15],[15,25],[0,1],[31,15],[26,15],[31,17],[15,5],[20,15],[0,28],[25,19],[15,12],[15,13],[26,27],[15,26],[15,1],[15,6],[15,25],[22,5],[11,20],[15,26],[2,15],[15,12],[24,15],[10,18],[15,21],[15,17],[15,18],[19,25],[14,0],[12,15],[15,25],[15,20],[15,23],[15,30],[15,24],[6,11],[6,15],[15,31],[13,15],[15,31],[7,15],[25,15],[19,0],[11,15],[23,25],[20,15],[15,28],[18,30],[15,27],[8,9],[0,15],[24,15],[15,23],[15,25],[15,14],[12,15],[15,6],[15,16],[15,26],[21,12],[23,15],[26,1],[25,15],[15,17],[30,15],[15,8],[25,30],[15,6],[5,15],[23,15],[15,2],[16,29],[15,13],[15,8],[9,28],[15,13],[8,15],[15,9],[31,16],[13,5],[15,25],[29,7],[15,23],[15,17],[8,15],[24,10],[0,15],[20,15],[15,27],[15,11],[15,10],[15,7],[3,10],[12,7],[15,3],[10,17],[14,9],[15,11],[15,1],[15,16],[15,21],[15,22],[1,24],[15,21],[13,7],[5,26],[15,29],[15,21],[27,15],[15,21],[15,11],[23,10],[31,15],[24,10],[7,15],[1,10],[8,16],[15,28]],[[15,24],[15,1],[15,24],[13,26],[15,0],[15,2],[29,17],[15,14],[15,26],[9,15],[22,15],[15,16],[8,18],[15,28],[25,11],[15,8],[15,17],[27,15],[10,20],[18,11],[15,20],[13,15],[15,22],[15,16],[29,15],[24,15],[0,23],[15,9],[15,0],[15,0],[4,2],[20,13],[15,17],[21,2],[3,26],[21,5],[30,15],[17,24],[15,22],[15,9],[13,16],[11,15],[12,15],[8,15],[12,15],[22,11],[15,22],[10,20],[6,15],[15,27],[15,26],[15,5],[15,11],[12,24],[18,15],[15,26],[28,30],[18,15],[21,15],[15,3],[18,2],[7,13],[21,15],[15,30],[2,18],[16,15],[2,15],[15,31],[11,27],[15,30],[18,14],[3,28],[17,15],[15,13],[15,27],[31,25],[28,21],[9,15],[10,24],[15,14],[15,6],[15,10],[30,29],[15,12],[15,13],[15,22],[15,18],[26,15],[23,14],[17,15],[2,11],[15,9],[15,31],[21,15],[14,16],[26,3],[21,25],[0,13],[26,16],[7,26],[15,16],[0,19],[15,18],[12,27],[18,24],[9,20],[15,31],[31,8],[30,15],[15,14],[15,27],[15,12],[11,15],[16,1],[15,5],[8,15],[15,23],[11,21],[15,21],[2,20],[15,8],[15,28],[27,15],[15,7],[8,15],[15,21],[15,14],[13,14],[15,3],[16,29],[23,4],[15,26],[13,15],[6,15],[15,6],[15,21],[15,18],[15,5],[1,15],[5,20],[15,4],[15,19],[14,15],[8,11],[2,15],[23,27],[28,12],[11,18],[15,7],[26,1],[13,19],[31,9],[15,24],[25,15],[14,15],[30,15],[19,23],[6,25],[17,15],[15,21],[15,23],[6,15],[15,11],[15,12],[15,26],[15,3],[15,10],[27,15],[3,22],[11,15],[6,15],[13,8],[15,20],[15,14],[15,14],[15,0],[19,21],[15,21],[15,28],[27,15],[25,1],[15,26],[3,17],[7,15],[15,21],[15,16],[15,10],[2,3],[15,14],[14,15],[15,26],[23,27],[31,5],[14,15],[3,15],[27,26],[24,15],[15,30],[15,16],[3,11],[15,14],[15,27],[30,3],[15,28],[27,24],[21,13],[18,11],[7,25],[10,2],[23,15],[31,15],[12,15],[13,9],[16,28],[25,30],[15,4],[15,10],[9,15],[15,28],[15,31],[15,27],[17,15],[15,18],[15,19],[3,15],[17,15],[23,29],[15,5],[9,22],[20,15],[0,9],[9,22],[15,12],[15,8],[22,30],[6,14],[11,15],[4,15],[15,3],[27,15],[15,24],[15,7],[15,24],[15,28],[15,8],[15,0],[20,15],[14,9],[15,17],[29,15],[11,17],[3,12],[3,14],[23,15],[15,19],[4,12]],[[15,21],[16,15],[12,15],[31,26],[12,22],[15,0],[15,3],[15,27],[21,15],[15,13],[7,11],[15,26],[30,15],[15,22],[17,20],[15,4],[15,4],[18,7],[16,9],[12,1],[15,10],[15,6],[8,15],[1,15],[15,19],[25,15],[15,18],[15,11],[15,7],[15,8],[11,15],[10,9],[2,24],[15,16],[3,15],[11,15],[29,2],[7,17],[26,15],[6,1],[15,27],[13,15],[16,15],[15,8],[27,15],[15,0],[0,8],[23,10],[15,6],[28,15],[0,15],[15,2],[3,15],[15,4],[15,22],[20,21],[18,15],[6,15],[27,4],[25,29],[15,25],[17,15],[10,15],[14,22],[15,13],[15,3],[2,15],[15,29],[15,24],[15,13],[15,7],[16,24],[15,13],[15,26],[14,15],[5,15],[15,16],[15,17],[15,19],[26,7],[2,15],[15,25],[11,15],[31,15],[15,22],[15,9],[3,17],[7,15],[11,17],[3,15],[15,19],[15,11],[6,23],[15,1],[27,29],[15,29],[15,31],[15,17],[4,25],[0,15],[15,11],[15,29],[15,30],[11,22],[15,31],[23,25],[25,27],[15,1],[20,15],[15,19],[3,13],[2,5],[31,15],[24,27],[15,7],[20,15],[16,29],[15,24],[23,13],[15,3],[15,9],[15,23],[9,29],[3,27],[8,15],[15,31],[29,15],[22,24],[25,0],[6,15],[30,15],[15,26],[15,5],[5,15],[15,16],[15,28],[15,5],[29,23],[25,12],[15,30],[15,9],[21,30],[15,13],[19,16],[27,15],[15,3],[15,2],[20,24],[18,24],[25,15],[15,8],[25,15],[18,15],[15,10],[17,18],[15,4],[15,0],[15,17],[15,7],[22,5],[15,1],[15,25],[15,4],[15,25],[15,22],[15,2],[15,25],[6,13],[22,27],[15,29],[16,15],[0,15],[20,23],[1,15],[15,10],[15,18],[30,24],[25,7],[26,15],[2,15],[15,25],[15,21],[15,4],[15,20],[15,16],[15,3],[15,1],[12,15],[14,15],[29,8],[1,15],[31,11],[12,11],[31,15],[11,29],[15,31],[15,3],[12,15],[12,14],[15,28],[15,22],[15,1],[16,7],[15,2],[31,6],[13,31],[15,8],[13,28],[15,20],[15,30],[20,15],[1,4],[15,21],[15,31],[25,15],[15,4],[15,17],[3,15],[23,15],[0,15],[29,27],[15,23],[11,15],[15,5],[15,17],[15,18],[15,28],[25,15],[15,5],[3,7],[15,23],[17,15],[15,29],[30,15],[15,31],[5,15],[19,14],[15,1],[15,27],[9,13],[12,15],[15,7],[31,30],[15,11],[0,15],[15,5],[22,31],[27,18],[18,15],[31,24],[30,15],[15,22],[24,31],[9,20],[24,11],[17,12]],[[4,9],[6,1],[15,1],[15,22],[9,15],[15,20],[15,25],[15,27],[15,31],[15,22],[15,19],[1,15],[15,29],[14,15],[15,6],[15,20],[24,18],[17,15],[25,15],[21,9],[15,16],[4,15],[15,25],[27,5],[15,10],[28,31],[15,11],[15,12],[10,27],[15,9],[0,30],[25,3],[24,8],[26,17],[15,22],[14,31],[3,15],[15,23],[15,7],[25,24],[30,9],[20,1],[27,15],[15,12],[12,26],[26,13],[15,26],[15,7],[9,31],[27,15],[3,15],[9,28],[15,14],[23,10],[27,24],[15,13],[14,15],[28,13],[15,30],[15,31],[31,15],[15,21],[13,15],[13,15],[17,15],[23,15],[15,23],[0,15],[16,15],[15,28],[9,2],[25,15],[11,15],[3,29],[15,28],[15,31],[7,16],[1,10],[15,9],[28,0],[7,15],[15,7],[15,5],[27,15],[15,28],[12,15],[15,19],[27,12],[21,14],[14,15],[15,19],[0,4],[15,25],[17,15],[15,30],[14,10],[7,8],[15,12],[15,13],[15,30],[15,18],[15,16],[21,10],[2,21],[31,15],[8,15],[0,15],[15,25],[24,15],[29,15],[2,22],[31,20],[3,24],[15,8],[15,16],[15,29],[31,18],[0,15],[26,15],[1,15],[31,14],[15,29],[26,15],[30,15],[18,26],[12,15],[19,2],[15,9],[15,3],[29,17],[4,15],[12,0],[28,15],[15,16],[8,13],[14,15],[15,6],[25,15],[15,26],[15,30],[15,9],[9,21],[0,15],[20,27],[22,15],[2,15],[1,15],[5,0],[4,15],[15,2],[10,5],[15,14],[15,26],[1,15],[20,3],[11,20],[15,0],[15,23],[21,18],[30,15],[28,8],[6,15],[15,5],[5,15],[14,3],[27,15],[15,2],[9,15],[15,25],[7,15],[3,19],[16,15],[0,15],[20,15],[3,15],[15,26],[24,22],[28,7],[16,15],[28,31],[15,14],[18,27],[10,21],[5,15],[15,21],[11,10],[22,15],[30,1],[15,20],[19,27],[15,2],[21,12],[21,15],[15,31],[25,15],[14,31],[18,7],[13,15],[15,23],[5,15],[15,29],[31,9],[27,20],[15,18],[23,15],[6,28],[26,31],[15,30],[7,28],[29,15],[15,21],[29,2],[19,23],[15,16],[15,10],[16,22],[10,11],[27,15],[24,15],[29,15],[19,21],[15,4],[15,27],[29,27],[15,2],[15,28],[12,15],[15,30],[7,10],[15,5],[17,15],[1,15],[1,15],[7,14],[2,12],[15,6],[18,15],[15,31],[15,8],[15,13],[15,7],[15,7],[15,24],[0,9],[9,15],[15,29],[15,23],[15,1],[15,11],[26,15],[24,15],[15,28],[15,3],[21,9],[28,15],[15,10]],[[6,15],[15,22],[15,4],[20,5],[15,17],[8,15],[15,29],[15,22],[11,20],[28,15],[0,15],[15,4],[15,23],[28,18],[2,30],[4,15],[12,4],[15,11],[15,30],[11,21],[8,2],[11,2],[15,5],[15,21],[27,15],[18,15],[17,9],[15,10],[15,10],[30,15],[15,6],[15,20],[15,12],[15,8],[16,1],[30,19],[15,28],[2,10],[15,31],[18,15],[27,15],[27,15],[12,19],[3,15],[14,15],[15,31],[15,6],[15,21],[15,30],[15,31],[2,15],[15,27],[10,15],[15,5],[9,15],[15,18],[15,8],[15,12],[15,12],[17,15],[17,29],[15,17],[19,21],[26,21],[15,18],[15,6],[2,12],[15,27],[23,15],[15,1],[22,15],[25,8],[27,15],[15,23],[24,31],[2,15],[15,22],[15,12],[14,15],[15,1],[26,15],[15,13],[15,6],[15,13],[1,15],[15,22],[18,2],[11,15],[15,7],[15,22],[25,15],[15,12],[10,15],[15,11],[1,15],[23,6],[31,15],[3,19],[1,27],[27,17],[15,9],[20,1],[15,5],[6,1],[15,17],[21,15],[28,15],[0,17],[15,25],[15,2],[6,15],[17,25],[6,2],[12,4],[30,29],[15,9],[14,4],[15,12],[7,15],[15,30],[15,27],[10,4],[15,19],[22,15],[20,15],[25,15],[11,15],[15,6],[15,28],[15,25],[16,6],[21,23],[21,28],[10,15],[27,12],[15,9],[10,13],[19,15],[15,24],[15,21],[16,25],[15,17],[24,15],[15,31],[15,2],[15,26],[15,10],[26,30],[16,2],[2,0],[12,15],[15,23],[30,0],[15,9],[21,30],[15,19],[15,19],[15,9],[3,0],[15,20],[30,3],[15,3],[24,15],[15,19],[24,11],[15,29],[15,7],[15,14],[31,15],[4,21],[15,8],[28,27],[14,15],[15,20],[27,26],[15,6],[15,7],[3,15],[20,15],[21,15],[8,15],[28,15],[31,28],[16,15],[5,15],[15,21],[15,12],[1,15],[25,15],[15,13],[15,20],[14,15],[15,13],[15,30],[29,28],[8,3],[15,2],[15,26],[14,15],[15,16],[27,16],[11,23],[15,18],[2,14],[15,8],[15,9],[15,20],[17,15],[18,26],[15,28],[11,1],[15,3],[15,25],[29,30],[15,10],[22,2],[15,19],[15,31],[15,24],[28,25],[6,26],[14,20],[15,18],[15,2],[29,7],[7,15],[15,4],[15,30],[11,14],[15,20],[10,15],[2,15],[15,25],[23,7],[6,3],[15,27],[3,15],[14,15],[2,29],[17,12],[29,17],[29,15],[29,15],[15,4],[30,26],[6,30],[15,14],[4,15],[15,26],[24,4],[16,20],[15,4],[13,24],[16,21],[15,14],[29,30]],[[20,9],[15,13],[11,15],[15,29],[13,11],[22,30],[15,23],[15,27],[31,15],[15,10],[11,14],[6,15],[15,3],[15,23],[20,15],[4,15],[26,12],[7,15],[22,24],[17,25],[8,23],[26,15],[17,15],[23,11],[18,17],[26,14],[15,25],[7,1],[31,10],[15,12],[14,4],[28,8],[15,28],[10,29],[0,15],[14,22],[7,3],[15,2],[1,15],[30,4],[25,15],[7,21],[25,14],[15,13],[15,21],[15,0],[15,3],[31,15],[8,13],[15,17],[14,15],[15,29],[15,19],[15,5],[24,31],[13,15],[23,15],[16,9],[15,3],[16,3],[19,0],[15,11],[29,18],[28,11],[15,10],[15,25],[3,15],[15,19],[16,5],[23,15],[15,25],[15,8],[15,13],[28,4],[15,17],[15,19],[2,12],[15,29],[1,14],[29,14],[5,14],[10,16],[15,9],[15,4],[5,21],[25,15],[15,28],[22,8],[15,13],[17,11],[15,22],[15,4],[3,15],[27,24],[6,5],[15,2],[7,15],[25,23],[15,2],[15,3],[15,4],[15,30],[25,2],[15,3],[0,7],[18,0],[15,25],[15,0],[7,27],[15,30],[17,2],[15,9],[10,15],[13,15],[15,27],[31,15],[15,22],[8,15],[23,21],[15,12],[28,13],[15,13],[3,31],[23,9],[17,2],[11,31],[15,5],[15,23],[15,16],[15,12],[15,26],[15,19],[9,16],[22,15],[4,23],[15,27],[15,23],[15,14],[2,15],[15,27],[15,20],[14,2],[15,22],[24,4],[15,27],[20,15],[16,15],[18,3],[5,15],[10,15],[6,5],[26,5],[20,0],[15,12],[15,3],[9,14],[30,4],[15,1],[15,10],[28,7],[30,9],[15,2],[15,18],[15,19],[18,3],[27,13],[15,12],[9,15],[19,6],[0,26],[15,8],[8,15],[9,15],[29,15],[15,10],[19,3],[12,6],[15,29],[14,15],[1,11],[19,2],[15,25],[15,26],[15,28],[18,11],[15,11],[15,26],[27,25],[31,18],[15,7],[15,26],[6,15],[15,23],[2,12],[2,7],[15,31],[25,13],[15,10],[13,8],[9,30],[29,11],[15,17],[15,30],[1,15],[15,26],[13,15],[15,26],[25,4],[15,5],[20,25],[7,13],[17,21],[15,11],[24,21],[15,12],[15,12],[15,17],[1,20],[15,1],[26,7],[15,27],[15,26],[20,9],[27,15],[15,31],[14,6],[15,23],[15,17],[18,23],[0,20],[6,15],[15,24],[15,21],[16,3],[15,29],[15,3],[15,0],[30,9],[2,16],[21,13],[3,17],[15,10],[7,25],[10,15],[12,11],[26,2],[20,2],[12,4],[14,15],[2,18],[31,22],[15,22],[15,8],[20,15],[0,7],[15,8]],[[15,5],[18,2],[15,7],[15,2],[3,18],[3,15],[26,7],[8,15],[21,15],[15,16],[13,10],[15,26],[22,26],[22,15],[15,22],[13,15],[15,17],[15,29],[2,1],[10,22],[28,15],[15,1],[15,24],[24,14],[31,9],[16,11],[18,8],[22,23],[1,26],[15,30],[31,27],[15,1],[14,26],[15,28],[22,2],[2,6],[23,1],[15,4],[2,20],[15,26],[25,15],[30,9],[0,3],[21,18],[11,12],[15,12],[12,31],[15,19],[18,21],[12,14],[19,15],[15,17],[15,20],[15,28],[15,22],[15,17],[14,26],[1,15],[15,2],[0,19],[15,30],[15,30],[10,27],[28,14],[24,28],[15,26],[15,10],[1,11],[20,15],[17,15],[15,19],[10,15],[2,3],[15,4],[9,15],[15,2],[29,23],[15,8],[2,15],[29,15],[15,29],[4,15],[29,21],[1,25],[15,14],[1,8],[21,25],[19,15],[25,15],[15,16],[21,15],[24,15],[6,5],[15,19],[29,15],[15,29],[13,15],[15,25],[15,28],[9,15],[23,15],[15,20],[2,17],[31,30],[15,17],[0,17],[16,2],[8,15],[24,15],[15,16],[24,14],[26,15],[27,15],[12,24],[31,20],[30,15],[15,6],[9,25],[15,14],[18,17],[15,19],[15,31],[17,15],[26,16],[15,6],[17,15],[26,15],[15,21],[30,15],[15,17],[21,15],[0,15],[31,26],[15,27],[15,13],[15,6],[31,9],[1,3],[30,15],[15,13],[15,1],[22,9],[15,17],[15,19],[15,21],[6,2],[15,28],[15,17],[31,6],[16,15],[15,26],[15,29],[15,8],[15,29],[17,23],[1,15],[25,15],[16,15],[15,10],[15,7],[26,22],[31,15],[5,15],[1,24],[8,13],[2,3],[15,1],[10,5],[15,24],[15,18],[18,15],[5,29],[12,15],[7,15],[15,14],[11,24],[18,20],[15,31],[6,15],[1,20],[15,9],[15,31],[15,20],[15,17],[30,15],[31,8],[30,22],[15,29],[18,5],[15,21],[13,16],[29,15],[18,0],[15,6],[15,6],[15,4],[7,4],[15,18],[15,22],[15,29],[6,15],[15,31],[15,17],[15,16],[14,15],[15,5],[15,14],[1,24],[15,31],[6,30],[15,8],[15,21],[4,22],[15,27],[15,9],[4,1],[24,19],[28,15],[15,24],[0,9],[15,4],[15,17],[0,15],[28,14],[15,27],[14,26],[16,15],[26,19],[22,15],[21,15],[12,19],[23,15],[15,26],[15,9],[15,11],[9,7],[25,15],[27,9],[15,1],[6,2],[17,22],[15,13],[15,17],[28,15],[15,6],[15,16],[0,20],[15,0],[15,30],[18,20],[15,30],[15,2],[25,27],[30,25],[28,22],[15,10]],[[3,17],[15,10],[15,14],[3,2],[8,26],[0,11],[15,14],[15,20],[27,29],[19,22],[21,30],[15,20],[16,15],[15,21],[15,26],[30,16],[15,14],[15,17],[6,28],[15,5],[21,2],[15,19],[19,16],[15,30],[17,15],[15,18],[15,20],[15,7],[5,15],[22,30],[2,15],[26,14],[21,15],[8,15],[15,12],[6,30],[31,16],[28,15],[22,10],[0,15],[30,17],[16,28],[15,6],[15,24],[31,21],[17,15],[12,26],[15,31],[15,1],[28,15],[15,22],[15,26],[24,8],[15,24],[15,9],[0,26],[5,15],[15,2],[14,15],[15,17],[15,26],[15,21],[15,17],[14,12],[28,27],[26,11],[15,20],[15,6],[24,15],[29,27],[11,4],[7,10],[4,23],[29,14],[24,17],[12,21],[15,5],[20,15],[28,11],[15,13],[15,4],[17,19],[30,10],[15,24],[15,1],[15,1],[21,15],[15,2],[24,13],[22,27],[23,18],[15,31],[9,15],[15,9],[28,30],[21,15],[4,15],[19,15],[0,18],[15,29],[22,15],[15,31],[28,15],[15,3],[12,15],[5,15],[15,16],[15,7],[5,13],[17,7],[15,3],[15,5],[8,24],[27,15],[15,27],[16,15],[15,8],[20,31],[3,6],[14,27],[9,19],[15,18],[15,18],[24,6],[15,28],[15,27],[15,9],[12,23],[15,18],[15,24],[0,15],[16,28],[15,17],[6,19],[26,15],[0,12],[30,1],[15,7],[18,15],[15,21],[24,15],[20,29],[27,15],[15,1],[23,15],[15,29],[14,5],[15,25],[27,15],[6,15],[3,21],[13,15],[6,11],[21,20],[12,1],[15,26],[3,13],[9,15],[25,9],[15,17],[15,4],[9,15],[14,19],[12,15],[15,1],[15,25],[15,26],[15,21],[15,14],[24,5],[14,15],[15,4],[29,25],[9,15],[23,15],[9,15],[26,14],[22,5],[14,22],[15,25],[27,24],[31,15],[15,6],[6,15],[4,15],[14,16],[24,15],[15,22],[11,12],[15,8],[14,15],[6,8],[15,1],[12,2],[15,11],[25,15],[15,4],[15,18],[15,19],[7,31],[10,1],[17,11],[15,1],[7,28],[15,30],[15,8],[15,24],[15,7],[15,12],[12,15],[15,17],[15,16],[15,12],[15,21],[31,15],[13,24],[15,28],[15,17],[31,0],[8,23],[15,16],[15,5],[6,13],[15,3],[15,31],[15,21],[10,15],[15,3],[15,9],[15,26],[17,15],[15,28],[10,15],[4,15],[7,15],[15,27],[5,13],[15,14],[9,29],[15,26],[15,17],[15,26],[19,28],[0,15],[10,27],[15,18],[21,19],[5,14],[15,5],[15,26],[4,25],[29,3],[15,4],[15,21],[15,4],[16,2]],[[26,15],[6,23],[15,31],[15,8],[0,15],[15,3],[5,15],[15,10],[15,7],[15,14],[15,25],[15,1],[15,25],[4,26],[15,4],[15,23],[15,2],[21,23],[27,28],[15,25],[29,15],[23,2],[7,16],[15,13],[15,30],[21,13],[15,9],[15,29],[17,13],[15,0],[1,15],[1,23],[23,18],[15,0],[15,20],[15,6],[0,15],[0,15],[25,12],[15,30],[15,0],[19,9],[18,15],[28,15],[18,7],[24,20],[15,23],[18,15],[12,21],[3,15],[6,15],[15,19],[15,18],[16,15],[31,27],[15,1],[4,15],[15,21],[28,31],[15,16],[15,17],[6,21],[14,15],[15,28],[28,15],[27,21],[28,24],[30,15],[15,7],[26,17],[15,10],[15,26],[10,16],[1,15],[15,4],[5,15],[15,31],[23,15],[1,15],[15,25],[25,4],[9,8],[15,18],[26,20],[15,23],[18,15],[15,9],[15,25],[15,4],[29,15],[15,7],[31,15],[14,13],[20,15],[15,26],[19,0],[15,12],[3,15],[6,15],[21,11],[10,13],[20,10],[15,20],[15,17],[3,6],[12,15],[17,2],[15,17],[10,22],[27,15],[20,15],[15,4],[12,29],[6,15],[5,15],[15,16],[16,1],[15,24],[15,31],[20,15],[24,9],[15,25],[14,21],[15,29],[15,2],[8,15],[6,30],[15,25],[15,18],[19,8],[17,15],[15,11],[15,8],[20,15],[26,15],[14,15],[4,7],[4,12],[28,19],[15,19],[16,14],[15,1],[10,25],[15,1],[12,23],[21,15],[9,15],[16,15],[16,29],[28,15],[15,31],[15,26],[18,15],[15,4],[15,5],[15,3],[15,16],[0,19],[25,15],[0,15],[15,10],[16,1],[15,21],[9,15],[9,2],[11,15],[15,4],[15,22],[17,20],[15,14],[30,4],[15,5],[13,15],[16,15],[15,28],[22,15],[15,20],[15,6],[1,29],[14,15],[15,11],[21,15],[15,31],[11,12],[29,12],[15,31],[26,15],[27,0],[22,15],[0,16],[17,9],[25,15],[15,25],[15,9],[18,8],[18,22],[28,10],[15,24],[15,3],[5,15],[30,22],[23,15],[30,15],[15,17],[0,28],[4,20],[26,15],[15,8],[15,0],[15,19],[2,15],[19,16],[15,23],[15,27],[13,15],[15,14],[30,15],[15,3],[13,30],[11,6],[19,11],[15,16],[26,31],[15,4],[7,15],[14,15],[30,15],[7,15],[7,15],[20,13],[27,6],[15,30],[13,15],[26,15],[15,17],[15,19],[29,23],[23,21],[15,22],[15,9],[15,21],[15,7],[15,4],[31,15],[15,16],[15,18],[31,30],[21,27],[4,15],[22,7],[15,16],[15,11],[20,10],[14,12],[30,15],[30,13]],[[20,12],[15,20],[31,4],[29,15],[5,24],[5,9],[15,7],[8,16],[15,23],[25,15],[21,31],[19,18],[13,7],[15,27],[31,15],[15,25],[20,15],[20,21],[20,8],[20,2],[16,15],[15,31],[15,2],[15,30],[13,0],[30,28],[7,15],[14,15],[15,14],[19,25],[29,7],[1,14],[1,15],[31,7],[15,20],[13,17],[15,0],[23,9],[3,15],[15,8],[10,4],[26,15],[12,15],[27,29],[26,21],[15,12],[22,15],[5,18],[29,15],[15,27],[15,22],[1,23],[15,28],[30,15],[11,8],[21,29],[31,27],[31,21],[2,10],[4,27],[29,15],[29,15],[15,18],[15,28],[24,31],[1,15],[19,4],[15,20],[8,16],[31,8],[4,2],[4,15],[3,23],[15,1],[29,8],[15,11],[9,5],[16,7],[17,15],[16,15],[10,15],[15,18],[20,30],[7,15],[30,1],[15,31],[16,8],[14,15],[13,15],[31,27],[30,8],[23,26],[28,12],[15,20],[15,31],[15,31],[16,22],[2,14],[15,10],[31,15],[6,0],[18,12],[15,24],[6,25],[12,19],[8,15],[25,15],[2,24],[1,19],[27,15],[24,0],[20,15],[15,6],[15,9],[15,31],[12,15],[28,23],[24,15],[0,28],[6,15],[5,26],[15,2],[15,3],[15,22],[4,28],[7,18],[24,19],[0,1],[12,15],[15,0],[30,18],[15,0],[5,15],[15,1],[19,20],[15,7],[15,17],[31,15],[3,15],[20,15],[15,29],[20,15],[15,29],[8,15],[6,23],[0,14],[4,3],[15,13],[15,19],[26,22],[18,15],[5,15],[13,15],[15,11],[4,15],[15,17],[27,15],[23,20],[15,21],[15,26],[15,13],[15,28],[30,15],[21,19],[17,24],[5,15],[15,7],[15,11],[20,15],[15,31],[15,27],[15,30],[15,8],[12,24],[15,18],[16,15],[15,14],[2,30],[15,1],[29,14],[17,15],[2,18],[15,30],[29,22],[24,15],[15,26],[8,15],[15,20],[27,15],[14,15],[14,15],[3,19],[20,27],[27,26],[16,13],[26,15],[31,15],[10,15],[7,28],[15,3],[28,30],[15,30],[0,15],[15,4],[15,11],[15,24],[15,29],[6,28],[15,10],[16,15],[21,30],[15,21],[31,15],[15,29],[11,15],[17,12],[21,8],[15,18],[21,15],[8,15],[6,13],[19,30],[16,31],[15,16],[15,21],[15,19],[15,28],[5,15],[7,2],[15,2],[15,26],[19,15],[15,26],[15,16],[14,15],[21,15],[1,22],[15,18],[13,14],[29,15],[15,4],[19,26],[15,2],[20,9],[15,18],[15,26],[15,18],[8,15],[10,31],[10,0],[9,15],[15,11],[25,11],[15,12],[15,3],[7,31]],[[13,15],[16,15],[2,21],[15,27],[15,29],[21,24],[25,15],[17,10],[20,15],[19,18],[0,29],[28,15],[0,15],[12,15],[15,31],[27,23],[15,1],[15,11],[20,1],[0,15],[22,9],[0,26],[26,15],[11,15],[15,11],[15,14],[6,15],[15,8],[15,6],[15,21],[15,0],[15,13],[31,28],[25,24],[22,12],[1,15],[15,6],[12,15],[14,0],[15,8],[15,17],[13,22],[18,15],[15,2],[15,8],[30,28],[23,6],[15,3],[15,24],[15,9],[15,14],[15,21],[15,31],[4,20],[16,15],[15,30],[18,15],[5,22],[15,17],[19,15],[28,29],[11,2],[29,15],[17,1],[15,11],[15,11],[26,11],[13,17],[20,11],[29,15],[15,20],[6,15],[2,7],[9,15],[15,29],[16,15],[9,8],[15,6],[14,6],[3,15],[15,14],[15,26],[13,15],[30,15],[15,0],[15,8],[15,27],[15,10],[15,6],[6,24],[15,27],[8,29],[26,14],[16,0],[13,15],[1,27],[19,15],[27,25],[15,23],[4,26],[15,20],[26,15],[30,15],[15,31],[2,15],[24,28],[15,7],[15,8],[15,5],[24,26],[15,11],[15,1],[6,10],[28,18],[2,1],[1,15],[15,29],[24,15],[3,15],[15,26],[29,3],[21,28],[25,15],[15,14],[0,12],[15,1],[19,15],[30,15],[15,22],[16,4],[15,23],[31,15],[2,19],[31,10],[15,12],[13,15],[14,22],[15,18],[29,15],[19,15],[19,14],[15,3],[8,14],[15,27],[17,15],[13,5],[31,15],[14,1],[15,8],[1,15],[29,15],[15,5],[31,15],[8,11],[15,1],[15,2],[15,19],[22,2],[18,31],[13,7],[18,15],[27,25],[1,16],[15,7],[29,24],[6,15],[12,21],[30,25],[15,12],[20,16],[19,18],[26,29],[25,15],[15,25],[15,8],[15,7],[24,2],[15,24],[19,15],[20,15],[15,19],[15,22],[15,21],[15,28],[15,5],[15,2],[13,15],[15,2],[2,4],[15,1],[0,23],[15,14],[15,7],[17,0],[26,15],[15,10],[15,3],[17,30],[7,9],[15,2],[15,13],[15,5],[5,15],[15,13],[15,14],[15,23],[15,14],[15,27],[15,16],[15,0],[22,10],[31,15],[21,17],[15,17],[21,17],[15,1],[15,29],[1,15],[15,13],[15,23],[15,13],[15,31],[17,16],[5,15],[15,25],[2,15],[15,4],[7,15],[15,3],[29,12],[15,25],[6,27],[15,19],[30,14],[5,18],[27,25],[1,31],[15,10],[15,19],[13,15],[15,11],[13,15],[14,19],[15,19],[15,30],[12,15],[15,10],[11,7],[26,15],[14,15],[15,7],[15,11],[10,14],[10,13],[13,16],[0,7]],[[15,14],[15,9],[29,15],[8,10],[15,0],[17,1],[15,31],[6,14],[30,14],[24,0],[27,30],[20,28],[9,21],[17,11],[15,26],[0,15],[15,29],[15,23],[15,6],[15,14],[15,22],[15,13],[15,9],[20,1],[13,1],[25,15],[17,31],[15,28],[6,19],[9,15],[29,15],[15,17],[23,15],[29,15],[4,15],[15,31],[30,16],[0,15],[15,8],[15,25],[3,21],[17,15],[15,25],[15,1],[27,15],[15,16],[17,22],[20,15],[16,15],[27,21],[13,15],[10,15],[24,12],[15,18],[2,15],[15,2],[15,29],[31,25],[2,15],[11,15],[15,16],[30,4],[15,6],[15,30],[15,19],[15,19],[1,15],[9,27],[15,10],[15,5],[22,15],[23,17],[16,3],[15,28],[29,28],[17,7],[0,16],[15,30],[22,9],[12,20],[19,17],[15,3],[5,11],[15,0],[5,29],[18,16],[30,15],[15,31],[14,15],[15,16],[15,24],[6,15],[27,21],[7,12],[3,15],[10,15],[28,15],[31,2],[15,7],[15,8],[15,26],[2,15],[15,1],[2,15],[6,21],[10,30],[15,26],[15,3],[1,0],[6,20],[24,1],[15,31],[15,28],[28,15],[10,15],[15,0],[24,15],[29,15],[17,15],[14,15],[19,26],[15,20],[15,3],[15,6],[9,18],[6,12],[26,2],[15,20],[15,5],[5,15],[15,9],[15,25],[1,15],[14,13],[3,27],[8,27],[23,15],[15,23],[15,11],[29,15],[15,25],[15,25],[28,15],[15,6],[19,15],[16,14],[30,24],[16,15],[15,26],[2,21],[15,26],[30,15],[2,12],[15,23],[15,16],[25,20],[8,15],[19,31],[15,17],[15,23],[15,20],[15,3],[19,21],[27,15],[10,15],[22,8],[2,0],[2,15],[31,5],[19,15],[15,16],[0,19],[31,11],[18,9],[15,25],[31,15],[15,12],[27,17],[25,12],[29,25],[31,6],[28,15],[15,25],[15,18],[14,15],[15,29],[15,13],[15,16],[28,10],[24,2],[15,26],[25,5],[7,15],[9,15],[1,25],[22,27],[27,15],[15,28],[21,15],[21,10],[27,3],[6,5],[15,3],[15,6],[6,18],[0,15],[13,7],[15,13],[5,7],[18,15],[21,19],[12,15],[15,30],[15,26],[15,12],[15,29],[15,4],[6,23],[15,6],[15,21],[15,24],[28,15],[14,15],[10,27],[12,15],[15,5],[27,13],[28,15],[15,11],[24,10],[15,2],[15,20],[16,22],[15,24],[15,0],[19,13],[5,11],[23,6],[29,15],[15,8],[2,15],[15,10],[15,28],[3,17],[19,15],[21,6],[15,16],[15,7],[1,2],[15,27],[14,11],[15,13],[1,14],[15,3],[25,9],[15,4]],[[29,4],[24,15],[18,15],[0,29],[25,6],[20,29],[15,2],[15,20],[25,15],[15,22],[17,29],[15,0],[15,1],[2,0],[27,15],[5,15],[15,11],[26,15],[17,1],[26,3],[14,16],[25,15],[15,8],[15,9],[15,17],[2,5],[10,19],[15,1],[15,27],[31,20],[15,5],[19,21],[15,9],[15,27],[3,4],[9,15],[15,13],[12,15],[5,24],[11,15],[15,16],[1,23],[21,14],[11,0],[27,14],[15,17],[15,1],[15,24],[8,15],[15,5],[2,3],[15,27],[15,9],[15,3],[14,26],[27,25],[15,14],[15,16],[1,31],[15,16],[22,15],[15,19],[2,15],[10,15],[10,15],[4,13],[16,25],[16,13],[15,18],[3,15],[1,6],[25,15],[15,1],[5,15],[15,21],[5,15],[15,26],[1,15],[15,17],[13,8],[0,25],[1,23],[15,31],[15,10],[30,11],[4,12],[15,0],[20,15],[15,6],[21,5],[15,19],[15,29],[15,14],[26,15],[24,23],[0,15],[15,16],[15,26],[18,10],[15,20],[28,4],[17,15],[2,4],[30,15],[20,25],[24,15],[29,14],[19,1],[15,6],[31,0],[15,9],[15,11],[12,15],[15,29],[30,3],[4,24],[15,2],[15,2],[15,3],[21,24],[27,21],[15,11],[22,18],[15,4],[27,16],[15,8],[31,24],[24,15],[27,7],[15,27],[5,18],[22,23],[15,10],[20,15],[15,25],[16,15],[15,2],[1,15],[15,27],[11,3],[15,16],[15,23],[0,15],[15,21],[1,15],[9,22],[17,2],[15,30],[15,28],[15,22],[15,18],[13,15],[12,15],[23,8],[8,22],[5,10],[15,4],[15,7],[15,29],[15,12],[22,29],[15,6],[12,24],[3,4],[15,4],[30,11],[15,25],[15,8],[15,16],[14,15],[15,25],[12,9],[4,15],[14,15],[15,4],[29,15],[15,8],[9,21],[10,31],[15,11],[16,1],[15,11],[25,15],[15,17],[15,3],[1,15],[8,30],[8,15],[23,15],[29,10],[15,23],[29,15],[24,15],[15,23],[15,0],[15,19],[21,15],[2,15],[15,8],[3,6],[15,9],[15,10],[3,15],[15,7],[1,15],[4,15],[15,24],[6,4],[11,20],[9,15],[2,15],[15,27],[15,12],[15,11],[30,15],[7,15],[15,31],[15,16],[15,21],[15,13],[13,25],[0,1],[15,3],[30,1],[15,28],[15,5],[15,12],[13,5],[11,15],[15,28],[6,17],[15,23],[29,22],[27,7],[29,30],[15,18],[16,15],[15,21],[27,11],[15,25],[15,7],[20,18],[15,27],[11,16],[4,16],[31,15],[14,13],[15,9],[23,15],[15,10],[15,29],[15,21],[18,20],[4,15],[5,15],[15,20]],[[29,15],[19,15],[11,15],[4,31],[4,15],[8,15],[15,27],[2,15],[15,11],[23,20],[15,1],[28,15],[15,9],[23,15],[20,10],[7,15],[10,15],[15,2],[15,10],[15,6],[15,5],[15,25],[0,15],[20,3],[15,29],[18,1],[29,15],[26,15],[23,6],[7,16],[19,10],[15,26],[3,4],[23,15],[2,15],[12,4],[15,17],[27,15],[15,26],[28,30],[15,4],[5,15],[15,29],[15,4],[15,26],[15,14],[1,28],[0,19],[15,5],[24,29],[22,16],[7,29],[15,10],[0,24],[15,0],[2,18],[20,15],[6,15],[21,15],[16,15],[15,7],[15,5],[15,30],[15,13],[15,17],[0,15],[15,22],[23,15],[16,15],[15,2],[15,7],[1,0],[11,15],[28,15],[19,9],[8,15],[1,15],[25,1],[16,15],[14,4],[10,15],[16,2],[28,15],[15,1],[15,19],[2,4],[18,24],[19,15],[6,15],[15,9],[24,30],[15,28],[29,23],[15,14],[15,0],[9,16],[8,22],[27,16],[15,19],[15,1],[2,18],[15,3],[15,19],[15,1],[12,11],[15,25],[15,14],[27,31],[15,9],[13,15],[15,10],[15,27],[15,17],[15,17],[18,14],[23,25],[24,15],[17,3],[15,5],[6,21],[27,6],[19,3],[15,4],[15,13],[6,27],[15,28],[4,3],[15,21],[21,0],[6,30],[25,9],[17,25],[20,9],[6,15],[1,24],[15,26],[15,4],[27,6],[15,1],[26,15],[13,15],[2,17],[15,14],[3,15],[14,0],[3,15],[15,24],[15,11],[5,21],[20,9],[5,15],[27,11],[16,10],[25,5],[15,11],[15,14],[15,19],[15,5],[6,25],[2,15],[5,15],[13,27],[15,20],[21,5],[31,22],[12,11],[15,16],[1,5],[30,15],[15,19],[26,14],[23,15],[15,21],[15,18],[20,24],[21,6],[15,23],[15,4],[1,15],[13,3],[15,10],[15,17],[15,25],[20,10],[5,28],[25,14],[1,28],[19,5],[7,31],[17,22],[15,13],[15,16],[15,17],[15,28],[15,6],[15,0],[10,17],[22,14],[25,15],[13,19],[15,23],[15,1],[14,15],[12,28],[7,15],[13,29],[4,15],[15,11],[6,4],[28,6],[4,22],[15,21],[15,0],[0,15],[24,20],[11,15],[1,15],[10,15],[21,28],[29,11],[20,26],[26,15],[15,30],[15,0],[25,15],[13,25],[15,29],[3,18],[15,13],[15,12],[29,4],[15,29],[15,22],[15,3],[15,10],[15,23],[29,15],[15,19],[14,15],[11,4],[15,9],[22,15],[22,10],[13,15],[15,25],[15,13],[15,26],[15,26],[15,10],[15,24],[15,18],[2,28],[27,15],[19,10],[15,1],[15,11]],[[15,7],[7,8],[14,15],[22,2],[24,19],[9,15],[9,1],[1,19],[15,1],[18,10],[15,25],[3,15],[15,0],[15,6],[15,13],[29,13],[8,23],[29,15],[23,15],[15,0],[15,18],[1,18],[15,0],[26,20],[15,22],[23,13],[11,7],[15,0],[25,15],[7,15],[15,8],[15,18],[26,3],[17,0],[25,15],[8,15],[27,4],[9,18],[22,15],[31,25],[15,5],[23,26],[15,29],[31,15],[11,15],[3,21],[24,15],[5,15],[31,15],[0,17],[15,3],[21,0],[15,4],[15,12],[15,22],[23,2],[21,15],[13,11],[16,23],[15,0],[15,14],[25,15],[15,1],[15,4],[30,15],[15,0],[8,23],[27,15],[27,15],[15,27],[15,10],[15,26],[10,15],[23,14],[11,21],[15,10],[23,1],[15,29],[29,30],[24,15],[15,28],[26,30],[31,9],[28,15],[29,15],[18,15],[15,5],[26,0],[15,29],[15,21],[24,12],[6,21],[18,15],[12,15],[10,6],[15,11],[27,11],[15,22],[9,4],[15,21],[15,6],[1,15],[6,30],[19,22],[27,15],[15,16],[15,14],[15,6],[6,20],[28,12],[15,29],[5,15],[24,14],[15,30],[15,14],[8,15],[15,13],[6,30],[30,15],[15,31],[15,13],[15,7],[10,15],[3,5],[8,24],[15,19],[14,27],[6,16],[27,15],[15,31],[27,15],[0,10],[15,14],[15,1],[15,27],[20,15],[15,6],[15,19],[16,23],[15,27],[15,23],[22,20],[0,10],[2,10],[11,10],[15,0],[29,30],[25,15],[19,15],[7,26],[15,11],[15,23],[15,23],[15,4],[21,7],[8,15],[21,15],[27,13],[15,19],[15,11],[15,19],[15,11],[23,15],[4,15],[13,1],[15,0],[15,27],[15,0],[15,27],[15,14],[15,18],[15,12],[12,1],[15,16],[2,21],[14,15],[31,15],[15,27],[15,17],[25,0],[15,10],[15,7],[15,28],[15,18],[2,15],[15,10],[15,8],[6,9],[18,15],[15,29],[15,6],[15,24],[27,15],[21,15],[16,15],[27,15],[24,30],[15,4],[15,4],[10,1],[17,15],[15,20],[15,27],[15,18],[15,1],[9,15],[0,15],[15,19],[10,15],[18,13],[15,4],[15,16],[13,14],[15,0],[15,6],[13,4],[17,5],[12,20],[8,17],[12,13],[15,20],[22,23],[13,18],[6,9],[15,7],[15,14],[0,10],[15,3],[8,15],[30,15],[17,15],[18,15],[15,17],[15,18],[15,8],[29,1],[27,15],[31,21],[15,2],[15,17],[1,15],[15,30],[14,20],[6,26],[15,5],[15,22],[15,31],[15,2],[31,15],[30,21],[5,25],[25,7],[16,17],[15,13],[15,7],[15,19]],[[15,5],[30,15],[19,21],[16,1],[26,15],[8,27],[15,8],[1,20],[15,4],[19,6],[0,15],[5,15],[15,1],[28,15],[15,13],[23,15],[3,17],[16,0],[15,18],[15,19],[15,6],[25,15],[31,15],[16,15],[15,16],[18,15],[15,2],[27,14],[15,20],[10,7],[13,8],[21,29],[7,10],[2,31],[6,24],[6,15],[16,30],[15,27],[16,15],[29,8],[30,15],[25,15],[31,24],[15,31],[26,15],[14,15],[15,3],[15,17],[21,9],[15,28],[15,4],[21,15],[15,14],[15,7],[30,16],[15,31],[8,15],[20,3],[15,19],[15,13],[28,12],[15,23],[15,12],[15,29],[31,19],[15,0],[15,18],[15,13],[15,23],[16,21],[9,30],[15,26],[1,10],[15,12],[15,9],[15,1],[17,15],[11,15],[4,15],[15,7],[15,12],[16,15],[12,15],[10,30],[10,16],[11,15],[15,27],[27,13],[15,7],[15,28],[2,3],[18,15],[31,3],[1,16],[25,15],[14,5],[13,15],[15,11],[15,29],[1,13],[12,13],[30,15],[31,15],[21,15],[15,5],[15,16],[0,6],[15,28],[27,15],[15,22],[15,29],[18,19],[15,19],[14,15],[12,15],[15,13],[15,6],[14,15],[6,11],[4,15],[18,15],[11,15],[8,15],[20,12],[15,2],[9,15],[15,7],[29,15],[15,8],[15,4],[13,15],[15,10],[30,15],[27,13],[20,12],[15,6],[15,12],[27,15],[15,1],[18,5],[30,15],[15,9],[26,15],[31,15],[0,15],[23,15],[8,15],[13,15],[15,26],[15,3],[15,18],[30,22],[17,26],[15,0],[6,15],[15,9],[15,14],[9,30],[10,15],[15,24],[26,10],[25,15],[15,21],[15,16],[6,5],[0,15],[15,5],[3,15],[29,15],[27,13],[15,6],[26,15],[26,24],[26,15],[15,17],[27,15],[15,23],[4,29],[15,28],[15,19],[15,28],[15,10],[15,28],[15,11],[15,7],[19,15],[15,29],[16,15],[15,0],[7,23],[15,8],[15,14],[20,15],[15,7],[18,15],[15,18],[15,1],[22,28],[15,24],[10,15],[26,31],[28,30],[15,17],[10,5],[13,28],[18,21],[10,22],[30,17],[15,26],[15,24],[15,26],[15,22],[27,23],[7,15],[0,19],[15,12],[15,31],[15,29],[16,31],[15,31],[28,31],[15,29],[6,15],[11,20],[15,8],[2,27],[15,5],[16,27],[15,9],[15,21],[17,20],[26,25],[15,24],[15,27],[15,11],[3,2],[29,7],[15,7],[12,18],[15,28],[19,15],[15,2],[28,19],[15,6],[15,7],[4,2],[15,20],[15,4],[21,7],[15,13],[7,15],[2,0],[5,15],[7,30],[15,10],[17,15]],[[28,23],[19,21],[12,14],[0,6],[22,29],[10,15],[27,11],[15,11],[11,23],[17,8],[17,15],[5,25],[22,15],[19,15],[15,17],[15,5],[18,7],[9,2],[15,19],[15,28],[15,4],[30,19],[15,10],[22,15],[18,15],[15,17],[30,17],[15,26],[1,15],[15,9],[15,27],[20,13],[15,14],[15,16],[15,27],[7,25],[15,7],[15,23],[7,15],[13,15],[15,18],[8,2],[25,16],[15,30],[15,11],[15,17],[17,15],[15,14],[17,15],[3,11],[15,0],[20,10],[15,9],[15,11],[28,15],[15,26],[27,23],[4,11],[2,14],[15,23],[15,26],[30,15],[15,19],[18,15],[15,12],[28,26],[15,27],[19,17],[7,15],[25,15],[31,15],[15,6],[11,16],[11,31],[23,9],[15,19],[15,30],[15,28],[15,22],[0,5],[15,24],[25,15],[1,15],[21,15],[15,9],[15,19],[15,31],[26,15],[30,18],[15,7],[19,6],[15,14],[15,13],[28,21],[21,15],[23,15],[24,17],[15,19],[24,15],[15,17],[15,31],[18,15],[15,20],[31,15],[18,25],[2,19],[15,0],[4,10],[2,16],[25,15],[25,15],[15,21],[19,0],[30,15],[15,27],[3,15],[8,15],[15,29],[10,11],[5,15],[13,17],[25,23],[15,4],[1,15],[15,6],[31,20],[15,27],[15,24],[15,14],[1,2],[15,8],[0,15],[11,6],[21,13],[10,14],[15,9],[18,15],[24,17],[2,27],[8,3],[6,7],[5,8],[19,14],[23,21],[4,15],[15,17],[15,19],[15,17],[17,15],[26,15],[15,8],[18,9],[15,31],[15,13],[25,15],[15,24],[15,6],[7,15],[15,29],[15,23],[15,22],[13,0],[7,31],[13,15],[16,21],[15,0],[13,15],[31,21],[0,2],[13,22],[10,15],[15,24],[15,4],[11,27],[1,23],[1,15],[21,28],[15,6],[15,28],[9,12],[15,12],[15,4],[28,15],[15,8],[5,13],[15,13],[22,15],[17,15],[15,1],[0,17],[28,15],[15,22],[15,31],[25,31],[20,24],[16,1],[29,15],[4,9],[15,12],[19,2],[16,17],[15,2],[20,15],[7,1],[29,5],[6,15],[15,2],[15,17],[15,6],[2,15],[15,25],[15,1],[15,10],[15,22],[15,19],[15,5],[16,31],[8,15],[15,3],[15,13],[15,31],[15,20],[15,28],[15,2],[15,10],[15,2],[16,18],[15,24],[15,14],[15,8],[15,9],[5,17],[11,15],[12,15],[16,15],[15,6],[15,1],[15,27],[26,15],[21,27],[15,8],[28,26],[15,0],[15,8],[20,29],[15,24],[15,11],[16,15],[30,15],[15,18],[15,12],[11,15],[15,8],[2,14],[15,1],[25,21]]]
CAP = 442
YW = 442
def setup_inputs(rng):
    return {"x": rng.standard_normal((N, 128, T), dtype=np.float32)}
def reference(x):
    y = np.full((N, 128, YW), np.nan, x.dtype)
    fill = [0] * N
    for r in range(N):
        for t in range(T):
            for e in ROUTE[r][t]:
                if fill[e] < CAP:
                    y[e][:, fill[e]] = x[r][:, t]
                fill[e] += 1
    return {"y": y}

@@ -1,0 +1,130 @@
+SCRATCH = {
+    "xs": ("sbuf", [128, 256], "float32"),
+    "pack": ("sbuf", [128, 512], "float32"),
+    "land": ("sbuf", [128, 442], "float32"),
+}
+SEMAPHORES = ["loaded", "packed", "own", "read", "handed", "arrived", "stored"]
+
+HELPERS = (2, 6, 3, 7)
+PLAN = {}
+
+
+def plan(T, topo):
+    if "p" in PLAN:
+        return PLAN["p"]
+    route, cap, cores = T.tables["ROUTE"], T.tables["CAP"], list(T.cores)
+    n = len(cores)
+    fill = [0] * n
+    toks = [[[] for e in range(n)] for r in range(n)]
+    off = [[0] * n for r in range(n)]
+    for r in range(n):
+        for e in range(n):
+            off[r][e] = min(fill[e], cap)
+        for t in range(len(route[r])):
+            for e in route[r][t]:
+                if fill[e] < cap:
+                    toks[r][e].append(t)
+                fill[e] += 1
+    count = [min(f, cap) for f in fill]
+    carriers = []
+    for r in range(n):
+        c = cores[r]
+        direct = [e for e in range(n) if e != r and toks[r][e] and topo.may_write(c, cores[e])]
+        cross = [e for e in range(n) if e != r and toks[r][e] and not topo.may_write(c, cores[e])]
+        loads = [[0, c - c % 8 + h, []] for h in HELPERS]
+        for e in sorted(cross, key=lambda e: -len(toks[r][e])):
+            b = min(loads, key=lambda l: l[0])
+            b[0] += len(toks[r][e])
+            b[2].append(e)
+        carriers.append([(c, direct)] + [(l[1], sorted(l[2])) for l in loads if l[2]])
+    pos = [[0] * n for r in range(n)]
+    span = []
+    for r in range(n):
+        p, s = 0, []
+        for (c, es) in carriers[r]:
+            a = p
+            for e in es:
+                pos[r][e] = p
+                p += len(toks[r][e])
+            s.append((a, p))
+        span.append(s)
+    arrive = [0] * n
+    for r in range(n):
+        for (c, es) in carriers[r]:
+            for e in es:
+                arrive[e] += 8
+    PLAN["p"] = dict(toks=toks, off=off, count=count, carriers=carriers, pos=pos, span=span, arrive=arrive)
+    return PLAN["p"]
+
+
+def runs(ts):
+    out = []
+    for i, t in enumerate(ts):
+        if out and out[-1][1] + out[-1][2] == t:
+            out[-1][2] += 1
+        else:
+            out.append([i, t, 1])
+    return out
+
+
+def send_blocks(g, core, T, topo, P, r, es):
+    k = 0
+    for e in es:
+        d = T.cores[e]
+        rid, pid = topo.addr(d, core)
+        w = len(P["toks"][r][e])
+        a, o = P["pos"][r][e], P["off"][r][e]
+        g.remote_dma(T.land[:, o:o + w], T.pack[:, a:a + w], remote_sem=T.sem.arrived, local_sem=T.sem.read,
+                     pid=pid, routing_id=rid, dma_engine_mask=0x00FF)
+        k += 8
+    return k
+
+
+def rank_program(g, core, T, topo):
+    P = plan(T, topo)
+    rank = T.rank_of(core)
+    if rank is None:
+        r = T.rank_of(core - core % 8 + 1)
+        if r is None:
+            return
+        for (c, es) in P["carriers"][r][1:]:
+            if c == core:
+                g.wait_ge(T.sem.handed, 16)
+                k = send_blocks(g, core, T, topo, P, r, es)
+                g.wait_ge(T.sem.read, k)
+        return
+
+    r = rank
+    g.sync.dma_start(T.xs[:], T.x[:]).then_inc(T.sem.loaded, 16)
+    g.sync.wait_ge(T.sem.loaded, 16)
+    g.scalar.wait_ge(T.sem.loaded, 16)
+    q = [g.sync, g.scalar]
+    k = 0
+    for (c, es) in P["carriers"][r]:
+        for e in es:
+            for (i, t, w) in runs(P["toks"][r][e]):
+                a = P["pos"][r][e] + i
+                q[k % 2].dma_start(T.pack[:, a:a + w], T.xs[:, t:t + w]).then_inc(T.sem.packed, 16)
+                k += 1
+    ko = 0
+    for (i, t, w) in runs(P["toks"][r][r]):
+        a = P["off"][r][r] + i
+        q[ko % 2].dma_start(T.land[:, a:a + w], T.xs[:, t:t + w]).then_inc(T.sem.own, 16)
+        ko += 1
+    g.wait_ge(T.sem.packed, 16 * k)
+    sent = 0
+    for j, (c, es) in enumerate(P["carriers"][r]):
+        if j == 0:
+            continue
+        a, b = P["span"][r][j]
+        rid, pid = topo.addr(c, core)
+        g.remote_dma(T.pack[:, a:b], T.pack[:, a:b], remote_sem=T.sem.handed, local_sem=T.sem.read,
+                     pid=pid, routing_id=rid, dma_engine_mask=0xFFFF)
+        sent += 16
+    sent += send_blocks(g, core, T, topo, P, r, P["carriers"][r][0][1])
+    g.wait_ge(T.sem.read, sent)
+    g.wait_ge(T.sem.own, 16 * ko)
+    g.wait_ge(T.sem.arrived, P["arrive"][r])
+    w = P["count"][r]
+    g.dma_start(T.y[:, 0:w], T.land[:, 0:w]).then_inc(T.sem.stored, 16)
+    g.wait_ge(T.sem.stored, 16)

@@ -1,12 +1,28 @@
+from concourse.bass import DstId, RemoteDMATransfer
+
+PIECE = 24
+PACKW = 85
+HOPW = 24
+NPK = 6
 SCRATCH = {
     "xs": ("sbuf", [128, 256], "float32"),
-    "pack": ("sbuf", [128, 512], "float32"),
+    "pack": ("sbuf", [128, PACKW], "float32"),
+    "hop": ("sbuf", [128, HOPW], "float32"),
     "land": ("sbuf", [128, 442], "float32"),
 }
-SEMAPHORES = ["loaded", "packed", "own", "read", "handed", "arrived", "stored"]
+SEMAPHORES = ["loaded", "shared", "own", "read", "hopped", "arrived", "stored"] + ["pk%d" % j for j in range(NPK)]
 
-HELPERS = (2, 6, 3, 7)
 PLAN = {}
+
+
+def runs(ts):
+    out = []
+    for i, t in enumerate(ts):
+        if out and out[-1][1] + out[-1][2] == t:
+            out[-1][2] += 1
+        else:
+            out.append([i, t, 1])
+    return out
 
 
 def plan(T, topo):
@@ -26,105 +42,207 @@ def plan(T, topo):
                     toks[r][e].append(t)
                 fill[e] += 1
     count = [min(f, cap) for f in fill]
-    carriers = []
-    for r in range(n):
-        c = cores[r]
-        direct = [e for e in range(n) if e != r and toks[r][e] and topo.may_write(c, cores[e])]
-        cross = [e for e in range(n) if e != r and toks[r][e] and not topo.may_write(c, cores[e])]
-        loads = [[0, c - c % 8 + h, []] for h in HELPERS]
-        for e in sorted(cross, key=lambda e: -len(toks[r][e])):
-            b = min(loads, key=lambda l: l[0])
-            b[0] += len(toks[r][e])
-            b[2].append(e)
-        carriers.append([(c, direct)] + [(l[1], sorted(l[2])) for l in loads if l[2]])
-    pos = [[0] * n for r in range(n)]
-    span = []
-    for r in range(n):
-        p, s = 0, []
-        for (c, es) in carriers[r]:
-            a = p
-            for e in es:
-                pos[r][e] = p
-                p += len(toks[r][e])
-            s.append((a, p))
-        span.append(s)
-    arrive = [0] * n
-    for r in range(n):
-        for (c, es) in carriers[r]:
-            for e in es:
-                arrive[e] += 8
-    PLAN["p"] = dict(toks=toks, off=off, count=count, carriers=carriers, pos=pos, span=span, arrive=arrive)
-    return PLAN["p"]
+    on_chip = dict((cores[r] // 8, r) for r in range(n))
+    mate = [on_chip[(cores[r] // 8) ^ 1] for r in range(n)]
+    cross = [[topo.chip(cores[r]) % 2 != topo.chip(cores[e]) % 2 for e in range(n)] for r in range(n)]
+    own_die = [topo.die(c) for c in cores]
 
+    pieces, cut = [], {}
+    for r in range(n):
+        for e in range(n):
+            w = len(toks[r][e])
+            if e == r or not w:
+                continue
+            k = -(-w // PIECE)
+            for j in range(k):
+                p = (r, e, w * j // k, w * (j + 1) // k)
+                pieces.append(p)
+                cut[p] = k > 1
 
-def runs(ts):
-    out = []
-    for i, t in enumerate(ts):
-        if out and out[-1][1] + out[-1][2] == t:
-            out[-1][2] += 1
+    def links(p, way):
+        r, e = p[0], p[1]
+        if way[0]:
+            return [("out", r, own_die[r]), ("in", mate[e], own_die[r]), ("mate", mate[e], way[1])]
+        if not cross[r][e]:
+            return [("out", r, way[1]), ("in", e, way[1])]
+        if mate[r] == e:
+            return [("mate", r, way[1])]
+        return [("mate", r, way[1]), ("out", mate[r], way[1]), ("in", e, way[1])]
+
+    load = {}
+    intake = [count[e] - len(toks[e][e]) for e in range(n)]
+
+    def put(p, way, sign):
+        w = (p[3] - p[2]) * sign
+        for k in links(p, way):
+            load[k] = load.get(k, 0) + w
+        if way[0]:
+            intake[mate[p[1]]] += w
+
+    def price(p, way):
+        w = p[3] - p[2]
+        return sum((load.get(k, 0) + w) ** 2 - load.get(k, 0) ** 2 for k in links(p, way))
+
+    def ways(p):
+        o = [(False, 0), (False, 1)]
+        r, e = p[0], p[1]
+        if cut[p] and cross[r][e] and mate[r] != e and intake[mate[e]] + p[3] - p[2] <= cap:
+            o += [(True, 0), (True, 1)]
+        return o
+
+    way = {}
+    for p in sorted(pieces, key=lambda p: (p[2] - p[3], p)):
+        way[p] = min(ways(p), key=lambda o: price(p, o))
+        put(p, way[p], 1)
+    for sweep in range(30):
+        moved = 0
+        for p in pieces:
+            old = way[p]
+            put(p, old, -1)
+            way[p] = min([old] + ways(p), key=lambda o: price(p, o))
+            put(p, way[p], 1)
+            moved += way[p] != old
+        if not moved:
+            break
+
+    busy, work, able = {}, {}, {}
+    for r in range(n):
+        for i in range(8):
+            busy[cores[r] - cores[r] % 8 + i] = 0
+            work[cores[r] - cores[r] % 8 + i] = []
+        busy[cores[r]] = len(runs(toks[r][r])) + 9
+
+    def cost(p):
+        return len(runs(toks[p[0]][p[1]][p[2]:p[3]])) + 1
+
+    order = sorted(pieces, key=lambda p: (not way[p][0], not cross[p[0]][p[1]], -cost(p), p))
+    for p in order:
+        c1 = cores[p[0]]
+        if way[p][0]:
+            can = [c1]
         else:
-            out.append([i, t, 1])
-    return out
-
-
-def send_blocks(g, core, T, topo, P, r, es):
-    k = 0
-    for e in es:
-        d = T.cores[e]
-        rid, pid = topo.addr(d, core)
-        w = len(P["toks"][r][e])
-        a, o = P["pos"][r][e], P["off"][r][e]
-        g.remote_dma(T.land[:, o:o + w], T.pack[:, a:a + w], remote_sem=T.sem.arrived, local_sem=T.sem.read,
-                     pid=pid, routing_id=rid, dma_engine_mask=0x00FF)
-        k += 8
-    return k
+            can = [c for c in range(c1 - c1 % 8, c1 - c1 % 8 + 8)
+                   if topo.die(c) == way[p][1] and topo.may_write(c, cores[p[1]])]
+        c = min(can, key=lambda c: (busy[c], c))
+        busy[c] += cost(p)
+        work[c].append(p)
+        able[p] = can
+    for sweep in range(30):
+        moved = 0
+        for c in sorted(work):
+            for c2 in range(c - c % 8, c - c % 8 + 8):
+                for p in list(work[c]):
+                    for q in [None] + list(work[c2]):
+                        d = cost(p) - (cost(q) if q else 0)
+                        if c2 in able[p] and (not q or c in able[q]) and p in work[c] and 0 < d < busy[c] - busy[c2]:
+                            work[c].remove(p)
+                            work[c2].append(p)
+                            if q:
+                                work[c2].remove(q)
+                                work[c].append(q)
+                            busy[c] -= d
+                            busy[c2] += d
+                            moved += 1
+        if not moved:
+            break
+    pos = {}
+    for c in work:
+        k = 0
+        for p in work[c]:
+            pos[p] = k
+            k += p[3] - p[2]
+        assert k <= PACKW and len(work[c]) <= NPK
+    via, hops, hpos = {}, dict((c, []) for c in work), {}
+    for p in order:
+        if way[p][0]:
+            c1 = cores[mate[p[1]]]
+            can = [c for c in range(c1 - c1 % 8, c1 - c1 % 8 + 8)
+                   if c != c1 and topo.die(c) == way[p][1] and topo.may_write(c, cores[p[1]])]
+            c = min(can, key=lambda c: (busy[c], c))
+            busy[c] += 1
+            via[p] = c
+            hpos[p] = sum(q[3] - q[2] for q in hops[c])
+            hops[c].append(p)
+            assert hpos[p] + p[3] - p[2] <= HOPW
+    arrive = [0] * n
+    for p in pieces:
+        arrive[p[1]] += 8
+    PLAN["p"] = dict(toks=toks, off=off, count=count, work=work, pos=pos, way=way, via=via, hops=hops, hpos=hpos,
+                     arrive=arrive, load=load, busy=busy, intake=intake)
+    return PLAN["p"]
 
 
 def rank_program(g, core, T, topo):
     P = plan(T, topo)
-    rank = T.rank_of(core)
-    if rank is None:
-        r = T.rank_of(core - core % 8 + 1)
-        if r is None:
-            return
-        for (c, es) in P["carriers"][r][1:]:
-            if c == core:
-                g.wait_ge(T.sem.handed, 16)
-                k = send_blocks(g, core, T, topo, P, r, es)
-                g.wait_ge(T.sem.read, k)
+    if core not in P["work"]:
         return
-
-    r = rank
-    g.sync.dma_start(T.xs[:], T.x[:]).then_inc(T.sem.loaded, 16)
-    g.sync.wait_ge(T.sem.loaded, 16)
-    g.scalar.wait_ge(T.sem.loaded, 16)
+    toks, off = P["toks"], P["off"]
+    rank = T.rank_of(core)
     q = [g.sync, g.scalar]
+    read = 0
+
+    if rank is not None:
+        g.sync.dma_start(T.xs[:], T.x[:]).then_inc(T.sem.loaded, 16)
+        for u in (g, g.sync, g.scalar):
+            u.wait_ge(T.sem.loaded, 16)
+        others = [c for c in range(core - core % 8, core - core % 8 + 8) if c != core]
+        ids = [topo.addr(c, core) for c in others]
+        g.remote_dma_fused([RemoteDMATransfer(dst_ids=[DstId(rid=a[0], pnc=a[1]) for a in ids],
+                                              dma_engine_mask=0xFFFF, remote_sem=T.sem.shared,
+                                              srcs=[T.xs[:]], dsts=[T.xs[:] for a in ids], alu_op=0)],
+                           local_sem=T.sem.read)
+        read += 16
+    else:
+        for u in (g, g.sync, g.scalar):
+            u.wait_ge(T.sem.shared, 16)
+
     k = 0
-    for (c, es) in P["carriers"][r]:
-        for e in es:
-            for (i, t, w) in runs(P["toks"][r][e]):
-                a = P["pos"][r][e] + i
-                q[k % 2].dma_start(T.pack[:, a:a + w], T.xs[:, t:t + w]).then_inc(T.sem.packed, 16)
-                k += 1
-    ko = 0
-    for (i, t, w) in runs(P["toks"][r][r]):
-        a = P["off"][r][r] + i
-        q[ko % 2].dma_start(T.land[:, a:a + w], T.xs[:, t:t + w]).then_inc(T.sem.own, 16)
-        ko += 1
-    g.wait_ge(T.sem.packed, 16 * k)
-    sent = 0
-    for j, (c, es) in enumerate(P["carriers"][r]):
-        if j == 0:
-            continue
-        a, b = P["span"][r][j]
-        rid, pid = topo.addr(c, core)
-        g.remote_dma(T.pack[:, a:b], T.pack[:, a:b], remote_sem=T.sem.handed, local_sem=T.sem.read,
-                     pid=pid, routing_id=rid, dma_engine_mask=0xFFFF)
-        sent += 16
-    sent += send_blocks(g, core, T, topo, P, r, P["carriers"][r][0][1])
-    g.wait_ge(T.sem.read, sent)
-    g.wait_ge(T.sem.own, 16 * ko)
-    g.wait_ge(T.sem.arrived, P["arrive"][r])
-    w = P["count"][r]
-    g.dma_start(T.y[:, 0:w], T.land[:, 0:w]).then_inc(T.sem.stored, 16)
-    g.wait_ge(T.sem.stored, 16)
+    picked = []
+    for j, p in enumerate(P["work"][core]):
+        rs = runs(toks[p[0]][p[1]][p[2]:p[3]])
+        for (i, t, w) in rs:
+            a = P["pos"][p] + i
+            q[k % 2].dma_start(T.pack[:, a:a + w], T.xs[:, t:t + w]).then_inc(T.sem["pk%d" % j], 16)
+            k += 1
+        picked.append(16 * len(rs))
+    own = 0
+    if rank is not None:
+        for (i, t, w) in runs(toks[rank][rank]):
+            a = off[rank][rank] + i
+            q[k % 2].dma_start(T.land[:, a:a + w], T.xs[:, t:t + w]).then_inc(T.sem.own, 16)
+            k += 1
+            own += 16
+
+    for j, p in enumerate(P["work"][core]):
+        g.wait_ge(T.sem["pk%d" % j], picked[j])
+        w = p[3] - p[2]
+        a = P["pos"][p]
+        if P["way"][p][0]:
+            d, o = P["via"][p], P["hpos"][p]
+            out, sem = T.hop[:, o:o + w], T.sem.hopped
+        else:
+            d, o = T.cores[p[1]], off[p[0]][p[1]] + p[2]
+            out, sem = T.land[:, o:o + w], T.sem.arrived
+        rid, pid = topo.addr(d, core)
+        g.remote_dma(out, T.pack[:, a:a + w], remote_sem=sem, local_sem=T.sem.read,
+                     pid=pid, routing_id=rid, dma_engine_mask=0x00FF)
+        read += 8
+
+    if P["hops"][core]:
+        g.wait_ge(T.sem.hopped, 8 * len(P["hops"][core]))
+        for p in P["hops"][core]:
+            w = p[3] - p[2]
+            a, o = P["hpos"][p], off[p[0]][p[1]] + p[2]
+            rid, pid = topo.addr(T.cores[p[1]], core)
+            g.remote_dma(T.land[:, o:o + w], T.hop[:, a:a + w], remote_sem=T.sem.arrived, local_sem=T.sem.read,
+                         pid=pid, routing_id=rid, dma_engine_mask=0x00FF)
+            read += 8
+    g.wait_ge(T.sem.read, read)
+
+    if rank is not None:
+        if own:
+            g.wait_ge(T.sem.own, own)
+        g.wait_ge(T.sem.arrived, P["arrive"][rank])
+        w = P["count"][rank]
+        g.dma_start(T.y[:, 0:w], T.land[:, 0:w]).then_inc(T.sem.stored, 16)
+        g.wait_ge(T.sem.stored, 16)

from concourse.bass import DstId, RemoteDMATransfer

PIECE = 24
PACKW = 85
HOPW = 24
NPK = 6
SCRATCH = {
    "xs": ("sbuf", [128, 256], "float32"),
    "pack": ("sbuf", [128, PACKW], "float32"),
    "hop": ("sbuf", [128, HOPW], "float32"),
    "land": ("sbuf", [128, 442], "float32"),
}
SEMAPHORES = ["loaded", "shared", "own", "read", "hopped", "arrived", "stored"] + ["pk%d" % j for j in range(NPK)]

PLAN = {}


def runs(ts):
    out = []
    for i, t in enumerate(ts):
        if out and out[-1][1] + out[-1][2] == t:
            out[-1][2] += 1
        else:
            out.append([i, t, 1])
    return out


def plan(T, topo):
    if "p" in PLAN:
        return PLAN["p"]
    route, cap, cores = T.tables["ROUTE"], T.tables["CAP"], list(T.cores)
    n = len(cores)
    fill = [0] * n
    toks = [[[] for e in range(n)] for r in range(n)]
    off = [[0] * n for r in range(n)]
    for r in range(n):
        for e in range(n):
            off[r][e] = min(fill[e], cap)
        for t in range(len(route[r])):
            for e in route[r][t]:
                if fill[e] < cap:
                    toks[r][e].append(t)
                fill[e] += 1
    count = [min(f, cap) for f in fill]
    on_chip = dict((cores[r] // 8, r) for r in range(n))
    mate = [on_chip[(cores[r] // 8) ^ 1] for r in range(n)]
    cross = [[topo.chip(cores[r]) % 2 != topo.chip(cores[e]) % 2 for e in range(n)] for r in range(n)]
    own_die = [topo.die(c) for c in cores]

    pieces, cut = [], {}
    for r in range(n):
        for e in range(n):
            w = len(toks[r][e])
            if e == r or not w:
                continue
            k = -(-w // PIECE)
            for j in range(k):
                p = (r, e, w * j // k, w * (j + 1) // k)
                pieces.append(p)
                cut[p] = k > 1

    def links(p, way):
        r, e = p[0], p[1]
        if way[0]:
            return [("out", r, own_die[r]), ("in", mate[e], own_die[r]), ("mate", mate[e], way[1])]
        if not cross[r][e]:
            return [("out", r, way[1]), ("in", e, way[1])]
        if mate[r] == e:
            return [("mate", r, way[1])]
        return [("mate", r, way[1]), ("out", mate[r], way[1]), ("in", e, way[1])]

    load = {}
    intake = [count[e] - len(toks[e][e]) for e in range(n)]

    def put(p, way, sign):
        w = (p[3] - p[2]) * sign
        for k in links(p, way):
            load[k] = load.get(k, 0) + w
        if way[0]:
            intake[mate[p[1]]] += w

    def price(p, way):
        w = p[3] - p[2]
        return sum((load.get(k, 0) + w) ** 2 - load.get(k, 0) ** 2 for k in links(p, way))

    def ways(p):
        o = [(False, 0), (False, 1)]
        r, e = p[0], p[1]
        if cut[p] and cross[r][e] and mate[r] != e and intake[mate[e]] + p[3] - p[2] <= cap:
            o += [(True, 0), (True, 1)]
        return o

    way = {}
    for p in sorted(pieces, key=lambda p: (p[2] - p[3], p)):
        way[p] = min(ways(p), key=lambda o: price(p, o))
        put(p, way[p], 1)
    for sweep in range(30):
        moved = 0
        for p in pieces:
            old = way[p]
            put(p, old, -1)
            way[p] = min([old] + ways(p), key=lambda o: price(p, o))
            put(p, way[p], 1)
            moved += way[p] != old
        if not moved:
            break

    busy, work, able = {}, {}, {}
    for r in range(n):
        for i in range(8):
            busy[cores[r] - cores[r] % 8 + i] = 0
            work[cores[r] - cores[r] % 8 + i] = []
        busy[cores[r]] = len(runs(toks[r][r])) + 9

    def cost(p):
        return len(runs(toks[p[0]][p[1]][p[2]:p[3]])) + 1

    order = sorted(pieces, key=lambda p: (not way[p][0], not cross[p[0]][p[1]], -cost(p), p))
    for p in order:
        c1 = cores[p[0]]
        if way[p][0]:
            can = [c1]
        else:
            can = [c for c in range(c1 - c1 % 8, c1 - c1 % 8 + 8)
                   if topo.die(c) == way[p][1] and topo.may_write(c, cores[p[1]])]
        c = min(can, key=lambda c: (busy[c], c))
        busy[c] += cost(p)
        work[c].append(p)
        able[p] = can
    for sweep in range(30):
        moved = 0
        for c in sorted(work):
            for c2 in range(c - c % 8, c - c % 8 + 8):
                for p in list(work[c]):
                    for q in [None] + list(work[c2]):
                        d = cost(p) - (cost(q) if q else 0)
                        if c2 in able[p] and (not q or c in able[q]) and p in work[c] and 0 < d < busy[c] - busy[c2]:
                            work[c].remove(p)
                            work[c2].append(p)
                            if q:
                                work[c2].remove(q)
                                work[c].append(q)
                            busy[c] -= d
                            busy[c2] += d
                            moved += 1
        if not moved:
            break
    pos = {}
    for c in work:
        k = 0
        for p in work[c]:
            pos[p] = k
            k += p[3] - p[2]
        assert k <= PACKW and len(work[c]) <= NPK
    via, hops, hpos = {}, dict((c, []) for c in work), {}
    for p in order:
        if way[p][0]:
            c1 = cores[mate[p[1]]]
            can = [c for c in range(c1 - c1 % 8, c1 - c1 % 8 + 8)
                   if c != c1 and topo.die(c) == way[p][1] and topo.may_write(c, cores[p[1]])]
            c = min(can, key=lambda c: (busy[c], c))
            busy[c] += 1
            via[p] = c
            hpos[p] = sum(q[3] - q[2] for q in hops[c])
            hops[c].append(p)
            assert hpos[p] + p[3] - p[2] <= HOPW
    arrive = [0] * n
    for p in pieces:
        arrive[p[1]] += 8
    PLAN["p"] = dict(toks=toks, off=off, count=count, work=work, pos=pos, way=way, via=via, hops=hops, hpos=hpos,
                     arrive=arrive, load=load, busy=busy, intake=intake)
    return PLAN["p"]


def rank_program(g, core, T, topo):
    P = plan(T, topo)
    if core not in P["work"]:
        return
    toks, off = P["toks"], P["off"]
    rank = T.rank_of(core)
    q = [g.sync, g.scalar]
    read = 0

    if rank is not None:
        g.sync.dma_start(T.xs[:], T.x[:]).then_inc(T.sem.loaded, 16)
        for u in (g, g.sync, g.scalar):
            u.wait_ge(T.sem.loaded, 16)
        others = [c for c in range(core - core % 8, core - core % 8 + 8) if c != core]
        ids = [topo.addr(c, core) for c in others]
        g.remote_dma_fused([RemoteDMATransfer(dst_ids=[DstId(rid=a[0], pnc=a[1]) for a in ids],
                                              dma_engine_mask=0xFFFF, remote_sem=T.sem.shared,
                                              srcs=[T.xs[:]], dsts=[T.xs[:] for a in ids], alu_op=0)],
                           local_sem=T.sem.read)
        read += 16
    else:
        for u in (g, g.sync, g.scalar):
            u.wait_ge(T.sem.shared, 16)

    k = 0
    picked = []
    for j, p in enumerate(P["work"][core]):
        rs = runs(toks[p[0]][p[1]][p[2]:p[3]])
        for (i, t, w) in rs:
            a = P["pos"][p] + i
            q[k % 2].dma_start(T.pack[:, a:a + w], T.xs[:, t:t + w]).then_inc(T.sem["pk%d" % j], 16)
            k += 1
        picked.append(16 * len(rs))
    own = 0
    if rank is not None:
        for (i, t, w) in runs(toks[rank][rank]):
            a = off[rank][rank] + i
            q[k % 2].dma_start(T.land[:, a:a + w], T.xs[:, t:t + w]).then_inc(T.sem.own, 16)
            k += 1
            own += 16

    for j, p in enumerate(P["work"][core]):
        g.wait_ge(T.sem["pk%d" % j], picked[j])
        w = p[3] - p[2]
        a = P["pos"][p]
        if P["way"][p][0]:
            d, o = P["via"][p], P["hpos"][p]
            out, sem = T.hop[:, o:o + w], T.sem.hopped
        else:
            d, o = T.cores[p[1]], off[p[0]][p[1]] + p[2]
            out, sem = T.land[:, o:o + w], T.sem.arrived
        rid, pid = topo.addr(d, core)
        g.remote_dma(out, T.pack[:, a:a + w], remote_sem=sem, local_sem=T.sem.read,
                     pid=pid, routing_id=rid, dma_engine_mask=0x00FF)
        read += 8

    if P["hops"][core]:
        g.wait_ge(T.sem.hopped, 8 * len(P["hops"][core]))
        for p in P["hops"][core]:
            w = p[3] - p[2]
            a, o = P["hpos"][p], off[p[0]][p[1]] + p[2]
            rid, pid = topo.addr(T.cores[p[1]], core)
            g.remote_dma(T.land[:, o:o + w], T.hop[:, a:a + w], remote_sem=T.sem.arrived, local_sem=T.sem.read,
                         pid=pid, routing_id=rid, dma_engine_mask=0x00FF)
            read += 8
    g.wait_ge(T.sem.read, read)

    if rank is not None:
        if own:
            g.wait_ge(T.sem.own, own)
        g.wait_ge(T.sem.arrived, P["arrive"][rank])
        w = P["count"][rank]
        g.dma_start(T.y[:, 0:w], T.land[:, 0:w]).then_inc(T.sem.stored, 16)
        g.wait_ge(T.sem.stored, 16)
